import numpy as np
import ml_dtypes


def mxq(x, axis, fmt="e4m3"):
    dtype, down = {"e4m3": (ml_dtypes.float8_e4m3fn, 7), "e5m2": (ml_dtypes.float8_e5m2, 14)}[fmt]
    v = np.moveaxis(np.asarray(x, np.float32).astype(ml_dtypes.bfloat16).astype(np.float64), axis, -1)
    blocks = v.reshape(v.shape[:-1] + (-1, 32))
    amax = np.abs(blocks).max(-1, keepdims=True)
    byte = np.maximum(np.where(amax > 0, np.frexp(amax)[1] - 1 + 127, 0) - down, 1)
    scale = np.exp2(byte - 127.0)
    codes = (blocks / scale).astype(np.float32).astype(dtype).astype(np.float64)
    return np.moveaxis((codes * scale).reshape(v.shape), -1, axis)


WIDE = False


def mx_kscale(k):
    if not WIDE:
        return np.ones(k)
    levels = np.array([10, -10, 5, -5, 0])
    if k % 512:
        return np.exp2(np.random.permutation(np.resize(levels, k // 32))).repeat(32)
    a = np.empty((k // 512, 16))
    for p in range(k // 512):
        a[p, :8] = np.random.permutation(np.resize(levels, 8))
        for g in range(8):
            far = levels[np.abs(levels - a[p, g]) >= 10]
            a[p, g + 8] = far[np.random.randint(len(far))]
    return np.exp2(a.ravel()).repeat(32)


def f64(x):
    return np.asarray(x).astype(np.float64)


def striped(idx):
    return np.tile(idx.reshape(-1, 16).T, (8, 1)).astype(np.uint16)


def unstriped(offs):
    return offs[:16].T.reshape(-1).astype(np.int64)


def silu(v):
    return v / (1.0 + np.exp(-np.maximum(v, -700.0)))


K, T, S, H, N = 512, 2048, 1024, 1024, 512


def setup_inputs():
    n = np.random.standard_normal
    s = mx_kscale(K)[:, None]
    u = mx_kscale(H)
    return {
        "xT": (n((K, T)) * s).astype(np.float32),
        "w1": (n((K, H)) / np.sqrt(K) / s).astype(np.float32),
        "w3": (n((K, H)) / np.sqrt(K) / s * u).astype(np.float32),
        "w2": (n((H, N)) / np.sqrt(H) / u[:, None]).astype(np.float32),
        "offs": striped(np.sort(np.random.permutation(T)[:S])),
    }


def reference(xT, w1, w3, w2, offs):
    idx = unstriped(offs)
    xq = mxq(f64(xT)[:, idx], 0, "e4m3")
    h = silu(mxq(f64(w1), 0, "e4m3").T @ xq) * (mxq(f64(w3), 0, "e4m3").T @ xq)
    y = mxq(f64(w2), 0, "e4m3").T @ mxq(h, 0, "e4m3")
    return y

@@ -1,0 +1,230 @@
+from contextlib import ExitStack
+
+import concourse.mybir as mybir
+
+K, T, S, H, N = 512, 2048, 1024, 1024, 512
+
+F32 = mybir.dt.float32
+BF16 = mybir.dt.bfloat16
+U32 = mybir.dt.uint32
+U16 = mybir.dt.uint16
+U8 = mybir.dt.uint8
+FP8X4 = mybir.dt.float8_e4m3fn_x4
+COPY = mybir.ActivationFunctionType.Copy
+SILU = mybir.ActivationFunctionType.Silu
+MULT = mybir.AluOpType.mult
+
+P = 128
+PACK = 4
+PASS = P * PACK
+SLICE = 128
+FLOPS = 2 * S * (2 * K * H + H * N)
+
+
+def tile_picked_pick_glu_silu_srt_e_kernel(tc, xT, w1, w3, w2, offs, out):
+    nc = tc.nc
+    with ExitStack() as ctx:
+        keep = ctx.enter_context(tc.tile_pool(name="keep", bufs=1))
+        ring = ctx.enter_context(tc.tile_pool(name="ring", bufs=4))
+        acc = ctx.enter_context(tc.psum_pool(name="acc", bufs=4))
+
+        offsets = keep.tile([P, S // 16], U16, name="offsets")
+        warm = keep.tile([P, 1], F32, name="warm")
+        nc.vector.memset(warm[:], 0.0)
+        nc.scalar.activation(warm[:], warm[:], SILU)
+        all_bytes = keep.tile([P, T], U8, name="all_bytes", align_bytes=64)
+        nc.gpsimd.memset(all_bytes[:], 0)
+        all_words = keep.tile([P, T], U32, name="all_words", align_bytes=64)
+
+        sources = {}
+        for c in range(4):
+            sources["x%d" % c] = xT[:, c * 512 : (c + 1) * 512]
+        for g in range(2):
+            sources["w1_%d" % g] = w1[:, g * 512 : (g + 1) * 512]
+            sources["w3_%d" % g] = w3[:, g * 512 : (g + 1) * 512]
+            sources["w2_%d" % g] = w2[g * 512 : (g + 1) * 512, :]
+        raw = {}
+        for name in ["x0","x1","offs","x2","x3","w1_0","w3_0","w1_1","w3_1","w2_0","w2_1"]:
+            if name == "offs":
+                nc.sync.dma_start(offsets[:], offs)
+            else:
+                tile = keep.tile([P, PACK, 512], F32, name="raw_" + name, align_bytes=64)
+                nc.sync.dma_start(out=tile[:], in_=sources[name].rearrange("(p j) c -> p j c", j=PACK))
+                raw[name] = tile[:]
+
+        grouped = {}
+        codes = {}
+        scales = {}
+
+        def cast(name, shares, start=0):
+            if start == 0:
+                fresh = keep.tile([P, 2048], BF16, name="grouped_" + name, align_bytes=64)
+                grouped[name] = fresh
+            tile = grouped[name]
+            if name[:2] in ("w1", "w3"):
+                dst = tile[:].rearrange("p (t m j) -> p m j t", t=PACK, j=PACK)
+                src = raw[name].rearrange("p j (m t) -> p m j t", t=PACK)
+            else:
+                dst = tile[:].rearrange("p (c i j) -> p c j i", i=4, j=PACK)
+                src = raw[name].rearrange("p j (c i) -> p c j i", i=4)
+            for engine, count in shares:
+                part = slice(start, start + count)
+                if engine == "V":
+                    nc.vector.tensor_copy(out=dst[:, part], in_=src[:, part])
+                elif engine == "S":
+                    nc.scalar.activation(dst[:, part], src[:, part], COPY)
+                else:
+                    if name[:2] == "w2":
+                        cols = slice(start * 4, (start + count) * 4)
+                        flat_dst = tile[:].rearrange("p (c j) -> p c j", j=PACK)[:, cols]
+                        flat_src = raw[name].rearrange("p j c -> p c j")[:, cols]
+                    else:
+                        flat_dst = tile[:].rearrange("p (t m j) -> p t m j", t=PACK, j=PACK)[:, :, part]
+                        flat_src = raw[name].rearrange("p j (m t) -> p t m j", t=PACK)[:, :, part]
+                    nc.gpsimd.tensor_scalar(
+                        out=flat_dst, in0=flat_src, scalar1=1.0, scalar2=0.0, op0=MULT, op1=mybir.AluOpType.add
+                    )
+                start = start + count
+
+        def quantize(name):
+            if name[0] == "x":
+                cols = slice(int(name[1:]) * 512, (int(name[1:]) + 1) * 512)
+                nc.vector.quantize_mx(out=all_words[:, cols].bitcast(FP8X4), scales=all_bytes[:, cols], in_=grouped[name][:])
+            else:
+                code = keep.tile([P, 512], U32, name="codes_" + name, align_bytes=64)
+                scale = keep.tile([P, 512], U8, name="scales_" + name, align_bytes=64)
+                nc.vector.quantize_mx(out=code[:].bitcast(FP8X4), scales=scale[:], in_=grouped[name][:])
+                codes[name] = code
+                scales[name] = scale
+
+        picked_words = keep.tile([P, S], U32, name="picked_words", align_bytes=64)
+        picked_bytes = keep.tile([P, S], U8, name="picked_bytes", align_bytes=64)
+
+        def gather(picked, window, first, last):
+            reach = last + T - S
+            entries = offsets[:, first // 16 : last // 16]
+            nc.vector.tensor_copy(out=picked[:, first:last], in_=window[:, 0:reach].indirect(entries))
+
+        h_grouped = []
+        h_codes = []
+        h_scales = []
+        for g in range(2):
+            a = keep.tile([P, S, PACK], BF16, name="h_grouped%d" % g, align_bytes=64)
+            b = keep.tile([P, S], U32, name="h_codes%d" % g, align_bytes=64)
+            c = keep.tile([P, S], U8, name="h_scales%d" % g, align_bytes=64)
+            h_grouped.append(a)
+            h_codes.append(b)
+            h_scales.append(c)
+
+        def unit(g, s):
+            cols = slice(s * SLICE, (s + 1) * SLICE)
+            gate = acc.tile([P, PACK, SLICE], F32, name="gate", tag="gate")
+            up = acc.tile([P, PACK, SLICE], F32, name="up", tag="up")
+            for layer, bank in (("w1_%d", gate), ("w3_%d", up)):
+                for t in range(PACK):
+                    rows = slice(t * P, (t + 1) * P)
+                    nc.tensor.matmul_mx(
+                        out=bank[:, t, :],
+                        lhsT=codes[layer % g][:, rows].bitcast(FP8X4),
+                        lhsT_scale=scales[layer % g][:, rows],
+                        rhs=picked_words[:, cols].bitcast(FP8X4),
+                        rhs_scale=picked_bytes[:, cols],
+                        start=True,
+                        stop=True,
+                    )
+            act = ring.tile([P, SLICE, PACK], F32, name="act")
+            nc.scalar.activation(act[:], gate[:].rearrange("p t n -> p n t"), SILU)
+            nc.vector.tensor_tensor(out=h_grouped[g][:, cols, :], in0=up[:].rearrange("p t n -> p n t"), in1=act[:], op=MULT)
+
+        def quantize_h(g, first, last):
+            nc.vector.quantize_mx(
+                out=h_codes[g][:, first:last].bitcast(FP8X4),
+                scales=h_scales[g][:, first:last],
+                in_=h_grouped[g][:, first:last, :].rearrange("p n t -> p (n t)"),
+            )
+
+        y_banks = {}
+
+        def product(first, last, g):
+            for m in range(4):
+                rows = slice(m * P, (m + 1) * P)
+                if g == 0:
+                    bank = acc.tile([P, last - first], F32, name="y%d_%d" % (first, m), tag="gate" if m % 2 == 0 else "up")
+                    y_banks[first, m] = bank
+                nc.tensor.matmul_mx(
+                    out=y_banks[first, m][:],
+                    lhsT=codes["w2_%d" % g][:, rows].bitcast(FP8X4),
+                    lhsT_scale=scales["w2_%d" % g][:, rows],
+                    rhs=h_codes[g][:, first:last].bitcast(FP8X4),
+                    rhs_scale=h_scales[g][:, first:last],
+                    start=(g == 0),
+                    stop=(g == 1),
+                )
+
+        def store(first, last, engines):
+            for m, engine in enumerate(engines):
+                y = keep.tile([P, last - first], F32, name="y_out%d_%d" % (first, m))
+                if engine == "S":
+                    nc.scalar.copy(y[:], y_banks[first, m][:])
+                else:
+                    nc.vector.tensor_copy(out=y[:], in_=y_banks[first, m][:])
+                nc.sync.dma_start(out=out[m * P : (m + 1) * P, first:last], in_=y[:])
+
+        cast("x0", (("V", 64), ("S", 64)))
+        quantize("x0")
+        cast("x1", (("V", 44), ("S", 84)))
+        quantize("x1")
+        cast("x2", (("V", 44), ("S", 84)))
+        quantize("x2")
+        gather(picked_words, all_words, 0, 512)
+        gather(picked_bytes, all_bytes, 0, 512)
+        cast("x3", (("V", 32), ("S", 96)))
+        quantize("x3")
+        cast("w1_0", (("S", 128),))
+        quantize("w1_0")
+        gather(picked_words, all_words, 512, 1024)
+        cast("w3_0", (("V", 64), ("S", 64)))
+        quantize("w3_0")
+        unit(0, 0)
+        unit(0, 1)
+        gather(picked_bytes, all_bytes, 512, 1024)
+        cast("w1_1", (("V", 24), ("S", 36)))
+        cast("w1_1", (("S", 34),), 60)
+        unit(0, 2)
+        cast("w1_1", (("S", 34),), 94)
+        unit(0, 3)
+        quantize("w1_1")
+        cast("w3_1", (("V", 24), ("S", 36)))
+        unit(0, 4)
+        quantize_h(0, 0, 512)
+        cast("w3_1", (("S", 34),), 60)
+        unit(0, 5)
+        cast("w3_1", (("S", 34),), 94)
+        unit(0, 6)
+        quantize("w3_1")
+        unit(1, 0)
+        cast("w2_0", (("G", 32), ("G", 32), ("G", 32), ("G", 32)))
+        unit(1, 1)
+        unit(1, 2)
+        quantize("w2_0")
+        unit(1, 3)
+        cast("w2_1", (("G", 32), ("G", 32), ("G", 32), ("G", 32)))
+        unit(0, 7)
+        quantize_h(1, 0, 512)
+        unit(1, 4)
+        quantize("w2_1")
+        quantize_h(0, 512, 1024)
+        product(0, 512, 0)
+        product(0, 512, 1)
+        unit(1, 5)
+        store(0, 512, "SVSV")
+        unit(1, 6)
+        quantize_h(1, 512, 768)
+        unit(1, 7)
+        product(512, 768, 0)
+        product(512, 768, 1)
+        store(512, 768, "SVSV")
+        product(768, 1024, 0)
+        quantize_h(1, 768, 1024)
+        product(768, 1024, 1)
+        store(768, 1024, "SVSV")

@@ -25,8 +25,8 @@ def tile_picked_pick_glu_silu_srt_e_kernel(tc, xT, w1, w3, w2, offs, out):
     nc = tc.nc
     with ExitStack() as ctx:
         keep = ctx.enter_context(tc.tile_pool(name="keep", bufs=1))
-        ring = ctx.enter_context(tc.tile_pool(name="ring", bufs=4))
-        acc = ctx.enter_context(tc.psum_pool(name="acc", bufs=4))
+        ring = ctx.enter_context(tc.tile_pool(name="ring", bufs=12))
+        acc = ctx.enter_context(tc.psum_pool(name="acc", bufs=3))
 
         offsets = keep.tile([P, S // 16], U16, name="offsets")
         warm = keep.tile([P, 1], F32, name="warm")
@@ -37,18 +37,19 @@ def tile_picked_pick_glu_silu_srt_e_kernel(tc, xT, w1, w3, w2, offs, out):
         all_words = keep.tile([P, T], U32, name="all_words", align_bytes=64)
 
         sources = {}
-        for c in range(4):
-            sources["x%d" % c] = xT[:, c * 512 : (c + 1) * 512]
+        token_cuts = (0, 512, 1024, 1280, 1536, 2048)
+        for c in range(len(token_cuts) - 1):
+            sources["x%d" % c] = xT[:, token_cuts[c] : token_cuts[c + 1]]
         for g in range(2):
             sources["w1_%d" % g] = w1[:, g * 512 : (g + 1) * 512]
             sources["w3_%d" % g] = w3[:, g * 512 : (g + 1) * 512]
             sources["w2_%d" % g] = w2[g * 512 : (g + 1) * 512, :]
         raw = {}
-        for name in ["x0","x1","offs","x2","x3","w1_0","w3_0","w1_1","w3_1","w2_0","w2_1"]:
+        for name in ["x0","x1","offs","x2","x3","x4","w1_0","w3_0","w1_1","w3_1","w2_0","w2_1"]:
             if name == "offs":
                 nc.sync.dma_start(offsets[:], offs)
             else:
-                tile = keep.tile([P, PACK, 512], F32, name="raw_" + name, align_bytes=64)
+                tile = keep.tile([P, PACK, sources[name].shape[1]], F32, name="raw_" + name, align_bytes=64)
                 nc.sync.dma_start(out=tile[:], in_=sources[name].rearrange("(p j) c -> p j c", j=PACK))
                 raw[name] = tile[:]
 
@@ -58,7 +59,7 @@ def tile_picked_pick_glu_silu_srt_e_kernel(tc, xT, w1, w3, w2, offs, out):
 
         def cast(name, shares, start=0):
             if start == 0:
-                fresh = keep.tile([P, 2048], BF16, name="grouped_" + name, align_bytes=64)
+                fresh = keep.tile([P, PACK * sources[name].shape[1]], BF16, name="grouped_" + name, align_bytes=64)
                 grouped[name] = fresh
             tile = grouped[name]
             if name[:2] in ("w1", "w3"):
@@ -88,7 +89,7 @@ def tile_picked_pick_glu_silu_srt_e_kernel(tc, xT, w1, w3, w2, offs, out):
 
         def quantize(name):
             if name[0] == "x":
-                cols = slice(int(name[1:]) * 512, (int(name[1:]) + 1) * 512)
+                cols = slice(token_cuts[int(name[1:])], token_cuts[int(name[1:]) + 1])
                 nc.vector.quantize_mx(out=all_words[:, cols].bitcast(FP8X4), scales=all_bytes[:, cols], in_=grouped[name][:])
             else:
                 code = keep.tile([P, 512], U32, name="codes_" + name, align_bytes=64)
@@ -116,25 +117,33 @@ def tile_picked_pick_glu_silu_srt_e_kernel(tc, xT, w1, w3, w2, offs, out):
             h_codes.append(b)
             h_scales.append(c)
 
-        def unit(g, s):
+        acts = {}
+
+        def hidden(layer, g, s, tag):
             cols = slice(s * SLICE, (s + 1) * SLICE)
-            gate = acc.tile([P, PACK, SLICE], F32, name="gate", tag="gate")
-            up = acc.tile([P, PACK, SLICE], F32, name="up", tag="up")
-            for layer, bank in (("w1_%d", gate), ("w3_%d", up)):
-                for t in range(PACK):
-                    rows = slice(t * P, (t + 1) * P)
-                    nc.tensor.matmul_mx(
-                        out=bank[:, t, :],
-                        lhsT=codes[layer % g][:, rows].bitcast(FP8X4),
-                        lhsT_scale=scales[layer % g][:, rows],
-                        rhs=picked_words[:, cols].bitcast(FP8X4),
-                        rhs_scale=picked_bytes[:, cols],
-                        start=True,
-                        stop=True,
-                    )
+            bank = acc.tile([P, PACK, SLICE], F32, name=tag, tag=tag, bufs=3)
+            for t in range(PACK):
+                rows = slice(t * P, (t + 1) * P)
+                nc.tensor.matmul_mx(
+                    out=bank[:, t, :],
+                    lhsT=codes[layer % g][:, rows].bitcast(FP8X4),
+                    lhsT_scale=scales[layer % g][:, rows],
+                    rhs=picked_words[:, cols].bitcast(FP8X4),
+                    rhs_scale=picked_bytes[:, cols],
+                    start=True,
+                    stop=True,
+                )
+            return bank[:].rearrange("p t n -> p n t")
+
+        def gate(g, s):
+            bank = hidden("w1_%d", g, s, "gate")
             act = ring.tile([P, SLICE, PACK], F32, name="act")
-            nc.scalar.activation(act[:], gate[:].rearrange("p t n -> p n t"), SILU)
-            nc.vector.tensor_tensor(out=h_grouped[g][:, cols, :], in0=up[:].rearrange("p t n -> p n t"), in1=act[:], op=MULT)
+            nc.scalar.activation(act[:], bank, SILU)
+            acts[g, s] = act
+
+        def up(g, s):
+            bank = hidden("w3_%d", g, s, "up")
+            nc.vector.tensor_tensor(out=h_grouped[g][:, s * SLICE : (s + 1) * SLICE, :], in0=bank, in1=acts[g, s][:], op=MULT)
 
         def quantize_h(g, first, last):
             nc.vector.quantize_mx(
@@ -145,86 +154,114 @@ def tile_picked_pick_glu_silu_srt_e_kernel(tc, xT, w1, w3, w2, offs, out):
 
         y_banks = {}
 
-        def product(first, last, g):
-            for m in range(4):
-                rows = slice(m * P, (m + 1) * P)
-                if g == 0:
-                    bank = acc.tile([P, last - first], F32, name="y%d_%d" % (first, m), tag="gate" if m % 2 == 0 else "up")
-                    y_banks[first, m] = bank
-                nc.tensor.matmul_mx(
-                    out=y_banks[first, m][:],
-                    lhsT=codes["w2_%d" % g][:, rows].bitcast(FP8X4),
-                    lhsT_scale=scales["w2_%d" % g][:, rows],
-                    rhs=h_codes[g][:, first:last].bitcast(FP8X4),
-                    rhs_scale=h_scales[g][:, first:last],
-                    start=(g == 0),
-                    stop=(g == 1),
-                )
+        def bank_tile(width, name, tag):
+            return acc.tile([P, width], F32, name=name, tag=tag, bufs=2 if tag == "y" else 3)
 
-        def store(first, last, engines):
+        def one_pass(dst, m, first, last, g):
+            rows = slice(m * P, (m + 1) * P)
+            nc.tensor.matmul_mx(
+                out=dst,
+                lhsT=codes["w2_%d" % g][:, rows].bitcast(FP8X4),
+                lhsT_scale=scales["w2_%d" % g][:, rows],
+                rhs=h_codes[g][:, first:last].bitcast(FP8X4),
+                rhs_scale=h_scales[g][:, first:last],
+                start=(g == 0),
+                stop=(g == 1),
+            )
+
+        def leave(bank, blocks, first, last, engine):
+            width = last - first
+            y = keep.tile([P, len(blocks), width], F32, name="y_out%d_%d" % (first, blocks[0]))
+            flat = y[:].rearrange("p m n -> p (m n)")
+            if engine == "S":
+                nc.scalar.copy(flat, bank[:])
+            else:
+                nc.vector.tensor_copy(out=flat, in_=bank[:])
+            rows = out[blocks[0] * P : (blocks[-1] + 1) * P, first:last]
+            nc.sync.dma_start(out=rows.rearrange("(m p) n -> p m n", p=P), in_=y[:])
+
+        def output(blocks, first, last, tag, engine):
+            width = last - first
+            bank = bank_tile(len(blocks) * width, "y%d_%d" % (first, blocks[0]), tag)
+            for place, m in enumerate(blocks):
+                for g in range(2):
+                    one_pass(bank[:, place * width : (place + 1) * width], m, first, last, g)
+            leave(bank, blocks, first, last, engine)
+
+        def open_output(first, last, tags):
+            for m, tag in enumerate(tags):
+                bank = bank_tile(last - first, "y%d_%d" % (first, m), tag)
+                y_banks[first, m] = bank
+                one_pass(bank[:], m, first, last, 0)
+
+        def close_output(first, last, engines):
             for m, engine in enumerate(engines):
-                y = keep.tile([P, last - first], F32, name="y_out%d_%d" % (first, m))
-                if engine == "S":
-                    nc.scalar.copy(y[:], y_banks[first, m][:])
-                else:
-                    nc.vector.tensor_copy(out=y[:], in_=y_banks[first, m][:])
-                nc.sync.dma_start(out=out[m * P : (m + 1) * P, first:last], in_=y[:])
+                one_pass(y_banks[first, m][:], m, first, last, 1)
+                leave(y_banks[first, m], (m,), first, last, engine)
 
         cast("x0", (("V", 64), ("S", 64)))
         quantize("x0")
-        cast("x1", (("V", 44), ("S", 84)))
+        cast("x1", (("V", 72), ("S", 56)))
         quantize("x1")
-        cast("x2", (("V", 44), ("S", 84)))
+        cast("x2", (("V", 40), ("S", 24)))
         quantize("x2")
-        gather(picked_words, all_words, 0, 512)
-        gather(picked_bytes, all_bytes, 0, 512)
-        cast("x3", (("V", 32), ("S", 96)))
+        cast("x3", (("S", 64),))
+        gather(picked_words, all_words, 0, 256)
+        gather(picked_bytes, all_bytes, 0, 256)
         quantize("x3")
+        gather(picked_words, all_words, 256, 512)
+        gather(picked_bytes, all_bytes, 256, 512)
+        cast("x4", (("S", 76), ("V", 52)))
+        quantize("x4")
         cast("w1_0", (("S", 128),))
-        quantize("w1_0")
         gather(picked_words, all_words, 512, 1024)
-        cast("w3_0", (("V", 64), ("S", 64)))
-        quantize("w3_0")
-        unit(0, 0)
-        unit(0, 1)
         gather(picked_bytes, all_bytes, 512, 1024)
-        cast("w1_1", (("V", 24), ("S", 36)))
-        cast("w1_1", (("S", 34),), 60)
-        unit(0, 2)
-        cast("w1_1", (("S", 34),), 94)
-        unit(0, 3)
+        quantize("w1_0")
+        cast("w3_0", (("S", 80), ("V", 48)))
+        for s in range(5):
+            gate(0, s)
+        quantize("w3_0")
+        cast("w1_1", (("V", 128),))
+        up(0, 0)
         quantize("w1_1")
-        cast("w3_1", (("V", 24), ("S", 36)))
-        unit(0, 4)
-        quantize_h(0, 0, 512)
-        cast("w3_1", (("S", 34),), 60)
-        unit(0, 5)
-        cast("w3_1", (("S", 34),), 94)
-        unit(0, 6)
+        cast("w3_1", (("S", 64),))
+        for s in range(4):
+            gate(1, s)
+        for s in range(1, 4):
+            up(0, s)
+        cast("w3_1", (("V", 64),), 64)
+        up(0, 4)
         quantize("w3_1")
-        unit(1, 0)
-        cast("w2_0", (("G", 32), ("G", 32), ("G", 32), ("G", 32)))
-        unit(1, 1)
-        unit(1, 2)
-        quantize("w2_0")
-        unit(1, 3)
-        cast("w2_1", (("G", 32), ("G", 32), ("G", 32), ("G", 32)))
-        unit(0, 7)
+        quantize_h(0, 0, 512)
+        gate(0, 5)
+        cast("w2_0", (("S", 64), ("S", 64)))
+        gate(0, 6)
+        cast("w2_1", (("S", 64), ("S", 64)))
+        for s in range(4):
+            up(1, s)
+        up(0, 5)
         quantize_h(1, 0, 512)
-        unit(1, 4)
+        quantize("w2_0")
+        gate(0, 7)
+        gate(1, 4)
+        up(0, 6)
         quantize("w2_1")
+        output((0,), 0, 512, "y", "S")
+        gate(1, 5)
+        up(0, 7)
+        output((1,), 0, 512, "y", "S")
+        gate(1, 6)
+        up(1, 4)
         quantize_h(0, 512, 1024)
-        product(0, 512, 0)
-        product(0, 512, 1)
-        unit(1, 5)
-        store(0, 512, "SVSV")
-        unit(1, 6)
+        output((2,), 0, 512, "y", "S")
+        gate(1, 7)
+        up(1, 5)
+        output((3,), 0, 512, "y", "S")
+        up(1, 6)
         quantize_h(1, 512, 768)
-        unit(1, 7)
-        product(512, 768, 0)
-        product(512, 768, 1)
-        store(512, 768, "SVSV")
-        product(768, 1024, 0)
+        up(1, 7)
+        output((0, 1), 512, 768, "y", "S")
+        open_output(768, 1024, ("gate", "gate", "gate", "up"))
         quantize_h(1, 768, 1024)
-        product(768, 1024, 1)
-        store(768, 1024, "SVSV")
+        output((2, 3), 512, 768, "y", "V")
+        close_output(768, 1024, "SVSV")

@@ -50,7 +50,12 @@ def tile_picked_pick_glu_silu_srt_e_kernel(tc, xT, w1, w3, w2, offs, out):
                 nc.sync.dma_start(offsets[:], offs)
             else:
                 tile = keep.tile([P, PACK, sources[name].shape[1]], F32, name="raw_" + name, align_bytes=64)
-                nc.sync.dma_start(out=tile[:], in_=sources[name].rearrange("(p j) c -> p j c", j=PACK))
+                if name[:2] == "w2":
+                    dealt = sources[name].rearrange("(q t e) c -> t q e c", t=PACK, e=2)
+                    for t in range(PACK):
+                        nc.sync.dma_start(out=tile[:, t, :], in_=dealt[t])
+                else:
+                    nc.sync.dma_start(out=tile[:], in_=sources[name].rearrange("(p j) c -> p j c", j=PACK))
                 raw[name] = tile[:]
 
         grouped = {}
@@ -63,28 +68,19 @@ def tile_picked_pick_glu_silu_srt_e_kernel(tc, xT, w1, w3, w2, offs, out):
                 grouped[name] = fresh
             tile = grouped[name]
             if name[:2] in ("w1", "w3"):
-                dst = tile[:].rearrange("p (t m j) -> p m j t", t=PACK, j=PACK)
-                src = raw[name].rearrange("p j (m t) -> p m j t", t=PACK)
+                dst = tile[:].rearrange("p (t q e j) -> p q t j e", t=PACK, e=2, j=PACK)
+                src = raw[name].rearrange("p j (q t e) -> p q t j e", t=PACK, e=2)
             else:
-                dst = tile[:].rearrange("p (c i j) -> p c j i", i=4, j=PACK)
-                src = raw[name].rearrange("p j (c i) -> p c j i", i=4)
+                dst = tile[:].rearrange("p (q t e j) -> p q t j e", t=PACK, e=2, j=PACK)
+                src = raw[name].rearrange("p j (q t e) -> p q t j e", t=PACK, e=2)
             for engine, count in shares:
                 part = slice(start, start + count)
                 if engine == "V":
                     nc.vector.tensor_copy(out=dst[:, part], in_=src[:, part])
-                elif engine == "S":
+                elif name[0] == "x":
                     nc.scalar.activation(dst[:, part], src[:, part], COPY)
                 else:
-                    if name[:2] == "w2":
-                        cols = slice(start * 4, (start + count) * 4)
-                        flat_dst = tile[:].rearrange("p (c j) -> p c j", j=PACK)[:, cols]
-                        flat_src = raw[name].rearrange("p j c -> p c j")[:, cols]
-                    else:
-                        flat_dst = tile[:].rearrange("p (t m j) -> p t m j", t=PACK, j=PACK)[:, :, part]
-                        flat_src = raw[name].rearrange("p j (m t) -> p t m j", t=PACK)[:, :, part]
-                    nc.gpsimd.tensor_scalar(
-                        out=flat_dst, in0=flat_src, scalar1=1.0, scalar2=0.0, op0=MULT, op1=mybir.AluOpType.add
-                    )
+                    nc.scalar.copy(dst[:, part], src[:, part])
                 start = start + count
 
         def quantize(name):
@@ -199,44 +195,44 @@ def tile_picked_pick_glu_silu_srt_e_kernel(tc, xT, w1, w3, w2, offs, out):
                 one_pass(y_banks[first, m][:], m, first, last, 1)
                 leave(y_banks[first, m], (m,), first, last, engine)
 
-        cast("x0", (("V", 64), ("S", 64)))
+        cast("x0", (("V", 32), ("S", 32)))
         quantize("x0")
-        cast("x1", (("V", 72), ("S", 56)))
+        cast("x1", (("V", 36), ("S", 28)))
         quantize("x1")
-        cast("x2", (("V", 40), ("S", 24)))
+        cast("x2", (("V", 20), ("S", 12)))
         quantize("x2")
-        cast("x3", (("S", 64),))
+        cast("x3", (("S", 32),))
         gather(picked_words, all_words, 0, 256)
         gather(picked_bytes, all_bytes, 0, 256)
         quantize("x3")
         gather(picked_words, all_words, 256, 512)
         gather(picked_bytes, all_bytes, 256, 512)
-        cast("x4", (("S", 76), ("V", 52)))
+        cast("x4", (("S", 38), ("V", 26)))
         quantize("x4")
-        cast("w1_0", (("S", 128),))
+        cast("w1_0", (("S", 64),))
         gather(picked_words, all_words, 512, 1024)
         gather(picked_bytes, all_bytes, 512, 1024)
         quantize("w1_0")
-        cast("w3_0", (("S", 80), ("V", 48)))
+        cast("w3_0", (("S", 40), ("V", 24)))
         for s in range(5):
             gate(0, s)
         quantize("w3_0")
-        cast("w1_1", (("V", 128),))
+        cast("w1_1", (("V", 64),))
         up(0, 0)
         quantize("w1_1")
-        cast("w3_1", (("S", 64),))
+        cast("w3_1", (("S", 32),))
         for s in range(4):
             gate(1, s)
         for s in range(1, 4):
             up(0, s)
-        cast("w3_1", (("V", 64),), 64)
+        cast("w3_1", (("V", 32),), 32)
         up(0, 4)
         quantize("w3_1")
         quantize_h(0, 0, 512)
         gate(0, 5)
-        cast("w2_0", (("S", 64), ("S", 64)))
+        cast("w2_0", (("S", 32), ("S", 32)))
         gate(0, 6)
-        cast("w2_1", (("S", 64), ("S", 64)))
+        cast("w2_1", (("S", 32), ("S", 32)))
         for s in range(4):
             up(1, s)
         up(0, 5)

@@ -37,7 +37,7 @@ def tile_picked_pick_glu_silu_srt_e_kernel(tc, xT, w1, w3, w2, offs, out):
         all_words = keep.tile([P, T], U32, name="all_words", align_bytes=64)
 
         sources = {}
-        token_cuts = (0, 512, 1024, 1280, 1536, 2048)
+        token_cuts = (0, 1024, 1536, 2048)
         for c in range(len(token_cuts) - 1):
             sources["x%d" % c] = xT[:, token_cuts[c] : token_cuts[c + 1]]
         for g in range(2):
@@ -45,7 +45,7 @@ def tile_picked_pick_glu_silu_srt_e_kernel(tc, xT, w1, w3, w2, offs, out):
             sources["w3_%d" % g] = w3[:, g * 512 : (g + 1) * 512]
             sources["w2_%d" % g] = w2[g * 512 : (g + 1) * 512, :]
         raw = {}
-        for name in ["x0","x1","offs","x2","x3","x4","w1_0","w3_0","w1_1","w3_1","w2_0","w2_1"]:
+        for name in ["x0","offs","x1","x2","w1_0","w3_0","w1_1","w3_1","w2_0","w2_1"]:
             if name == "offs":
                 nc.sync.dma_start(offsets[:], offs)
             else:
@@ -83,6 +83,43 @@ def tile_picked_pick_glu_silu_srt_e_kernel(tc, xT, w1, w3, w2, offs, out):
                     nc.scalar.copy(dst[:, part], src[:, part])
                 start = start + count
 
+        def cast_slots(name, engine, first, last):
+            if name not in grouped:
+                fresh = keep.tile([P, PACK * 512], BF16, name="grouped_" + name, align_bytes=64)
+                grouped[name] = fresh
+            dst = grouped[name][:].rearrange("p (t q e j) -> p q t j e", t=PACK, e=2, j=PACK)[:, :, first:last]
+            src = raw[name].rearrange("p j (q t e) -> p q t j e", t=PACK, e=2)[:, :, first:last]
+            if engine == "V":
+                nc.vector.tensor_copy(out=dst, in_=src)
+            else:
+                nc.scalar.copy(dst, src)
+
+        def cast_on_gpsimd(name, pieces):
+            fresh = keep.tile([P, PACK * 512], BF16, name="grouped_" + name, align_bytes=64)
+            grouped[name] = fresh
+            dst = fresh[:].rearrange("p (c j) -> p c j", j=PACK)
+            src = raw[name].rearrange("p j c -> p c j")
+            width = 512 // pieces
+            for piece in range(pieces):
+                part = slice(piece * width, (piece + 1) * width)
+                nc.gpsimd.tensor_scalar(
+                    out=dst[:, part], in0=src[:, part], scalar1=1.0, scalar2=0.0, op0=MULT, op1=mybir.AluOpType.add
+                )
+
+        def quantize_part(name, first, last):
+            values = grouped[name][:, first * PACK : last * PACK]
+            if name[0] == "x":
+                base = token_cuts[int(name[1:])]
+                cols = slice(base + first, base + last)
+                nc.vector.quantize_mx(out=all_words[:, cols].bitcast(FP8X4), scales=all_bytes[:, cols], in_=values)
+            else:
+                if name not in codes:
+                    code = keep.tile([P, 512], U32, name="codes_" + name, align_bytes=64)
+                    scale = keep.tile([P, 512], U8, name="scales_" + name, align_bytes=64)
+                    codes[name] = code
+                    scales[name] = scale
+                nc.vector.quantize_mx(out=codes[name][:, first:last].bitcast(FP8X4), scales=scales[name][:, first:last], in_=values)
+
         def quantize(name):
             if name[0] == "x":
                 cols = slice(token_cuts[int(name[1:])], token_cuts[int(name[1:]) + 1])
@@ -117,7 +154,7 @@ def tile_picked_pick_glu_silu_srt_e_kernel(tc, xT, w1, w3, w2, offs, out):
 
         def hidden(layer, g, s, tag):
             cols = slice(s * SLICE, (s + 1) * SLICE)
-            bank = acc.tile([P, PACK, SLICE], F32, name=tag, tag=tag, bufs=3)
+            bank = acc.tile([P, PACK, SLICE], F32, name=tag, tag=tag, bufs=2 if tag == "y" else 3)
             for t in range(PACK):
                 rows = slice(t * P, (t + 1) * P)
                 nc.tensor.matmul_mx(
@@ -137,8 +174,15 @@ def tile_picked_pick_glu_silu_srt_e_kernel(tc, xT, w1, w3, w2, offs, out):
             nc.scalar.activation(act[:], bank, SILU)
             acts[g, s] = act
 
-        def up(g, s):
-            bank = hidden("w3_%d", g, s, "up")
+        up_banks = {}
+
+        def up_product(g, s, tag="up"):
+            up_banks[g, s] = hidden("w3_%d", g, s, tag)
+
+        def up(g, s, tag="up"):
+            if (g, s) not in up_banks:
+                up_product(g, s, tag)
+            bank = up_banks[g, s]
             nc.vector.tensor_tensor(out=h_grouped[g][:, s * SLICE : (s + 1) * SLICE, :], in0=bank, in1=acts[g, s][:], op=MULT)
 
         def quantize_h(g, first, last):
@@ -153,7 +197,7 @@ def tile_picked_pick_glu_silu_srt_e_kernel(tc, xT, w1, w3, w2, offs, out):
         def bank_tile(width, name, tag):
             return acc.tile([P, width], F32, name=name, tag=tag, bufs=2 if tag == "y" else 3)
 
-        def one_pass(dst, m, first, last, g):
+        def one_pass(dst, m, first, last, g, opens):
             rows = slice(m * P, (m + 1) * P)
             nc.tensor.matmul_mx(
                 out=dst,
@@ -161,8 +205,8 @@ def tile_picked_pick_glu_silu_srt_e_kernel(tc, xT, w1, w3, w2, offs, out):
                 lhsT_scale=scales["w2_%d" % g][:, rows],
                 rhs=h_codes[g][:, first:last].bitcast(FP8X4),
                 rhs_scale=h_scales[g][:, first:last],
-                start=(g == 0),
-                stop=(g == 1),
+                start=opens,
+                stop=not opens,
             )
 
         def leave(bank, blocks, first, last, engine):
@@ -180,84 +224,87 @@ def tile_picked_pick_glu_silu_srt_e_kernel(tc, xT, w1, w3, w2, offs, out):
             width = last - first
             bank = bank_tile(len(blocks) * width, "y%d_%d" % (first, blocks[0]), tag)
             for place, m in enumerate(blocks):
-                for g in range(2):
-                    one_pass(bank[:, place * width : (place + 1) * width], m, first, last, g)
+                for g in (1, 0):
+                    one_pass(bank[:, place * width : (place + 1) * width], m, first, last, g, g == 1)
             leave(bank, blocks, first, last, engine)
 
         def open_output(first, last, tags):
             for m, tag in enumerate(tags):
                 bank = bank_tile(last - first, "y%d_%d" % (first, m), tag)
                 y_banks[first, m] = bank
-                one_pass(bank[:], m, first, last, 0)
+                one_pass(bank[:], m, first, last, 0, True)
 
         def close_output(first, last, engines):
             for m, engine in enumerate(engines):
-                one_pass(y_banks[first, m][:], m, first, last, 1)
+                one_pass(y_banks[first, m][:], m, first, last, 1, False)
                 leave(y_banks[first, m], (m,), first, last, engine)
 
-        cast("x0", (("V", 32), ("S", 32)))
-        quantize("x0")
-        cast("x1", (("V", 36), ("S", 28)))
-        quantize("x1")
-        cast("x2", (("V", 20), ("S", 12)))
-        quantize("x2")
-        cast("x3", (("S", 32),))
-        gather(picked_words, all_words, 0, 256)
-        gather(picked_bytes, all_bytes, 0, 256)
-        quantize("x3")
-        gather(picked_words, all_words, 256, 512)
-        gather(picked_bytes, all_bytes, 256, 512)
-        cast("x4", (("S", 38), ("V", 26)))
-        quantize("x4")
-        cast("w1_0", (("S", 64),))
+        cast("x0", (("V", 72), ("S", 56)))
+        quantize_part("x0", 0, 512)
+        quantize_part("x0", 512, 1024)
+        cast("x1", (("S", 24), ("V", 40)))
+        quantize_part("x1", 256, 512)
+        quantize_part("x1", 0, 256)
+        gather(picked_words, all_words, 0, 512)
+        gather(picked_bytes, all_bytes, 0, 512)
+        cast("x2", (("S", 32), ("S", 32)))
+        quantize_part("x2", 0, 256)
+        quantize_part("x2", 256, 512)
+        cast_slots("w1_0", "S", 0, 2)
+        cast_slots("w1_0", "S", 2, 4)
         gather(picked_words, all_words, 512, 1024)
         gather(picked_bytes, all_bytes, 512, 1024)
         quantize("w1_0")
-        cast("w3_0", (("S", 40), ("V", 24)))
+        cast_slots("w3_0", "S", 0, 2)
+        cast_slots("w3_0", "V", 3, 4)
+        cast_slots("w3_0", "S", 2, 3)
+        quantize_part("w3_0", 0, 256)
+        quantize_part("w3_0", 256, 512)
         for s in range(5):
             gate(0, s)
-        quantize("w3_0")
         cast("w1_1", (("V", 64),))
         up(0, 0)
         quantize("w1_1")
-        cast("w3_1", (("S", 32),))
         for s in range(4):
             gate(1, s)
         for s in range(1, 4):
             up(0, s)
-        cast("w3_1", (("V", 32),), 32)
+        cast("w3_1", (("V", 64),))
         up(0, 4)
         quantize("w3_1")
         quantize_h(0, 0, 512)
-        gate(0, 5)
         cast("w2_0", (("S", 32), ("S", 32)))
-        gate(0, 6)
-        cast("w2_1", (("S", 32), ("S", 32)))
+        gate(0, 5)
+        gate(1, 4)
+        gate(1, 5)
         for s in range(4):
             up(1, s)
-        up(0, 5)
-        quantize_h(1, 0, 512)
+        cast("w2_1", (("S", 32), ("V", 32)))
         quantize("w2_0")
-        gate(0, 7)
-        gate(1, 4)
-        up(0, 6)
+        quantize_h(1, 0, 512)
         quantize("w2_1")
-        output((0,), 0, 512, "y", "S")
-        gate(1, 5)
-        up(0, 7)
-        output((1,), 0, 512, "y", "S")
+        gate(0, 6)
+        gate(0, 7)
         gate(1, 6)
-        up(1, 4)
-        quantize_h(0, 512, 1024)
-        output((2,), 0, 512, "y", "S")
         gate(1, 7)
+        up(0, 5, "y")
+        up(1, 4)
         up(1, 5)
-        output((3,), 0, 512, "y", "S")
-        up(1, 6)
+        up_product(0, 6, "y")
+        up_product(0, 7, "y")
+        up_product(1, 6)
+        up_product(1, 7)
+        quantize_h(0, 512, 768)
+        for m in range(4):
+            output((m,), 0, 512, "gate", "SSSS"[m])
+        up(0, 6)
         quantize_h(1, 512, 768)
-        up(1, 7)
+        up(0, 7)
+        up(1, 6)
+        quantize_h(0, 768, 1024)
         output((0, 1), 512, 768, "y", "S")
-        open_output(768, 1024, ("gate", "gate", "gate", "up"))
+        output((2, 3), 512, 768, "gate", "S")
+        up(1, 7)
+        open_output(768, 1024, ("gate", "y", "up", "up"))
         quantize_h(1, 768, 1024)
-        output((2, 3), 512, 768, "y", "V")
-        close_output(768, 1024, "SVSV")
+        close_output(768, 1024, "VSVS")

@@ -49,7 +49,7 @@ def tile_picked_pick_glu_silu_srt_e_kernel(tc, xT, w1, w3, w2, offs, out):
             if name == "offs":
                 nc.sync.dma_start(offsets[:], offs)
             else:
-                tile = keep.tile([P, PACK, sources[name].shape[1]], F32, name="raw_" + name, align_bytes=64)
+                tile = keep.tile([P, PACK, sources[name].shape[1]], F32, name="raw_" + name, tag="raw_" + name, align_bytes=64)
                 if name[:2] == "w2":
                     dealt = sources[name].rearrange("(q t e) c -> t q e c", t=PACK, e=2)
                     for t in range(PACK):
@@ -139,11 +139,12 @@ def tile_picked_pick_glu_silu_srt_e_kernel(tc, xT, w1, w3, w2, offs, out):
             entries = offsets[:, first // 16 : last // 16]
             nc.vector.tensor_copy(out=picked[:, first:last], in_=window[:, 0:reach].indirect(entries))
 
+        H_OVER = ("raw_w1_1", "h_second")
         h_grouped = []
         h_codes = []
         h_scales = []
         for g in range(2):
-            a = keep.tile([P, S, PACK], BF16, name="h_grouped%d" % g, align_bytes=64)
+            a = keep.tile([P, S, PACK], BF16, name="h_grouped%d" % g, tag=H_OVER[g], align_bytes=64)
             b = keep.tile([P, S], U32, name="h_codes%d" % g, align_bytes=64)
             c = keep.tile([P, S], U8, name="h_scales%d" % g, align_bytes=64)
             h_grouped.append(a)
@@ -168,10 +169,19 @@ def tile_picked_pick_glu_silu_srt_e_kernel(tc, xT, w1, w3, w2, offs, out):
                 )
             return bank[:].rearrange("p t n -> p n t")
 
-        def gate(g, s):
+        reused = {}
+
+        def gate(g, s, over=None):
             bank = hidden("w1_%d", g, s, "gate")
-            act = ring.tile([P, SLICE, PACK], F32, name="act")
-            nc.scalar.activation(act[:], bank, SILU)
+            if over is None:
+                fresh = ring.tile([P, SLICE, PACK], F32, name="act")
+                act = fresh[:]
+            else:
+                if over not in reused:
+                    four = keep.tile([P, PACK, SLICE, PACK], F32, name="acts_" + over, tag="raw_" + over, align_bytes=64)
+                    reused[over] = four
+                act = reused[over][:, s % PACK]
+            nc.scalar.activation(act, bank, SILU)
             acts[g, s] = act
 
         up_banks = {}
@@ -183,7 +193,20 @@ def tile_picked_pick_glu_silu_srt_e_kernel(tc, xT, w1, w3, w2, offs, out):
             if (g, s) not in up_banks:
                 up_product(g, s, tag)
             bank = up_banks[g, s]
-            nc.vector.tensor_tensor(out=h_grouped[g][:, s * SLICE : (s + 1) * SLICE, :], in0=bank, in1=acts[g, s][:], op=MULT)
+            nc.vector.tensor_tensor(out=h_grouped[g][:, s * SLICE : (s + 1) * SLICE, :], in0=bank, in1=acts[g, s], op=MULT)
+
+        def warm_tensor(passes):
+            idle = acc.tile([P, 512], F32, name="idle", tag="y", bufs=2)
+            for turn in range(passes):
+                nc.tensor.matmul_mx(
+                    out=idle[:],
+                    lhsT=picked_words[:, 512:640].bitcast(FP8X4),
+                    lhsT_scale=picked_bytes[:, 0:128],
+                    rhs=picked_words[:, 0:512].bitcast(FP8X4),
+                    rhs_scale=picked_bytes[:, 0:512],
+                    start=True,
+                    stop=True,
+                )
 
         def quantize_h(g, first, last):
             nc.vector.quantize_mx(
@@ -234,17 +257,31 @@ def tile_picked_pick_glu_silu_srt_e_kernel(tc, xT, w1, w3, w2, offs, out):
                 y_banks[first, m] = bank
                 one_pass(bank[:], m, first, last, 0, True)
 
+        def close_in_pairs(first, last):
+            width = last - first
+            for pair in range(2):
+                y = keep.tile([P, 2, width], F32, name="y_last%d" % pair)
+                for place in range(2):
+                    m = 2 * pair + place
+                    one_pass(y_banks[first, m][:], m, first, last, 1, False)
+                    if place == 0:
+                        nc.scalar.copy(y[:, place, :], y_banks[first, m][:])
+                    else:
+                        nc.vector.tensor_copy(out=y[:, place, :], in_=y_banks[first, m][:])
+                rows = out[2 * pair * P : (2 * pair + 2) * P, first:last]
+                nc.sync.dma_start(out=rows.rearrange("(m p) n -> p m n", p=P), in_=y[:])
+
         def close_output(first, last, engines):
             for m, engine in enumerate(engines):
                 one_pass(y_banks[first, m][:], m, first, last, 1, False)
                 leave(y_banks[first, m], (m,), first, last, engine)
 
-        cast("x0", (("V", 72), ("S", 56)))
+        cast("x0", (("V", 64), ("S", 64)))
         quantize_part("x0", 0, 512)
         quantize_part("x0", 512, 1024)
-        cast("x1", (("S", 24), ("V", 40)))
-        quantize_part("x1", 256, 512)
+        cast("x1", (("S", 32), ("V", 32)))
         quantize_part("x1", 0, 256)
+        quantize_part("x1", 256, 512)
         gather(picked_words, all_words, 0, 512)
         gather(picked_bytes, all_bytes, 0, 512)
         cast("x2", (("S", 32), ("S", 32)))
@@ -253,6 +290,7 @@ def tile_picked_pick_glu_silu_srt_e_kernel(tc, xT, w1, w3, w2, offs, out):
         cast_slots("w1_0", "S", 0, 2)
         cast_slots("w1_0", "S", 2, 4)
         gather(picked_words, all_words, 512, 1024)
+        warm_tensor(3)
         gather(picked_bytes, all_bytes, 512, 1024)
         quantize("w1_0")
         cast_slots("w3_0", "S", 0, 2)
@@ -279,7 +317,7 @@ def tile_picked_pick_glu_silu_srt_e_kernel(tc, xT, w1, w3, w2, offs, out):
         gate(1, 5)
         for s in range(4):
             up(1, s)
-        cast("w2_1", (("S", 32), ("V", 32)))
+        cast("w2_1", (("S", 48), ("V", 16)))
         quantize("w2_0")
         quantize_h(1, 0, 512)
         quantize("w2_1")

@@ -132,12 +132,18 @@ def tile_picked_pick_glu_silu_srt_e_kernel(tc, xT, w1, w3, w2, offs, out):
                 scales[name] = scale
 
         picked_words = keep.tile([P, S], U32, name="picked_words", align_bytes=64)
-        picked_bytes = keep.tile([P, S], U8, name="picked_bytes", align_bytes=64)
+        early_bytes = keep.tile([P, S // 2], U8, name="early_bytes", align_bytes=64)
+        late_bytes = keep.tile([P, S // 2], U8, name="late_bytes", tag="raw_w1_0", align_bytes=64)
+        picked_bytes = (early_bytes, late_bytes)
 
         def gather(picked, window, first, last):
             reach = last + T - S
             entries = offsets[:, first // 16 : last // 16]
-            nc.vector.tensor_copy(out=picked[:, first:last], in_=window[:, 0:reach].indirect(entries))
+            if window is all_bytes:
+                dst = picked[first // 512][:]
+            else:
+                dst = picked[:, first:last]
+            nc.vector.tensor_copy(out=dst, in_=window[:, 0:reach].indirect(entries))
 
         H_OVER = ("raw_w1_1", "h_second")
         h_grouped = []
@@ -163,7 +169,7 @@ def tile_picked_pick_glu_silu_srt_e_kernel(tc, xT, w1, w3, w2, offs, out):
                     lhsT=codes[layer % g][:, rows].bitcast(FP8X4),
                     lhsT_scale=scales[layer % g][:, rows],
                     rhs=picked_words[:, cols].bitcast(FP8X4),
-                    rhs_scale=picked_bytes[:, cols],
+                    rhs_scale=picked_bytes[s // 4][:, (s % 4) * SLICE : (s % 4 + 1) * SLICE],
                     start=True,
                     stop=True,
                 )
@@ -201,9 +207,9 @@ def tile_picked_pick_glu_silu_srt_e_kernel(tc, xT, w1, w3, w2, offs, out):
                 nc.tensor.matmul_mx(
                     out=idle[:],
                     lhsT=picked_words[:, 512:640].bitcast(FP8X4),
-                    lhsT_scale=picked_bytes[:, 0:128],
+                    lhsT_scale=early_bytes[:, 0:128],
                     rhs=picked_words[:, 0:512].bitcast(FP8X4),
-                    rhs_scale=picked_bytes[:, 0:512],
+                    rhs_scale=early_bytes[:],
                     start=True,
                     stop=True,
                 )
@@ -243,12 +249,12 @@ def tile_picked_pick_glu_silu_srt_e_kernel(tc, xT, w1, w3, w2, offs, out):
             rows = out[blocks[0] * P : (blocks[-1] + 1) * P, first:last]
             nc.sync.dma_start(out=rows.rearrange("(m p) n -> p m n", p=P), in_=y[:])
 
-        def output(blocks, first, last, tag, engine):
+        def output(blocks, first, last, tag, engine, groups=(1, 0)):
             width = last - first
             bank = bank_tile(len(blocks) * width, "y%d_%d" % (first, blocks[0]), tag)
             for place, m in enumerate(blocks):
-                for g in (1, 0):
-                    one_pass(bank[:, place * width : (place + 1) * width], m, first, last, g, g == 1)
+                for g in groups:
+                    one_pass(bank[:, place * width : (place + 1) * width], m, first, last, g, g == groups[0])
             leave(bank, blocks, first, last, engine)
 
         def open_output(first, last, tags):
@@ -288,18 +294,20 @@ def tile_picked_pick_glu_silu_srt_e_kernel(tc, xT, w1, w3, w2, offs, out):
         quantize_part("x2", 0, 256)
         quantize_part("x2", 256, 512)
         cast_slots("w1_0", "S", 0, 2)
-        cast_slots("w1_0", "S", 2, 4)
+        cast_slots("w1_0", "S", 2, 3)
         gather(picked_words, all_words, 512, 1024)
-        warm_tensor(3)
+        cast_slots("w1_0", "V", 3, 4)
+        quantize_part("w1_0", 0, 256)
+        quantize_part("w1_0", 256, 512)
         gather(picked_bytes, all_bytes, 512, 1024)
-        quantize("w1_0")
         cast_slots("w3_0", "S", 0, 2)
         cast_slots("w3_0", "V", 3, 4)
         cast_slots("w3_0", "S", 2, 3)
         quantize_part("w3_0", 0, 256)
         quantize_part("w3_0", 256, 512)
-        for s in range(5):
-            gate(0, s)
+        for s in range(4):
+            gate(0, s, over="w3_0")
+        gate(0, 4)
         cast("w1_1", (("V", 64),))
         up(0, 0)
         quantize("w1_1")
@@ -311,20 +319,17 @@ def tile_picked_pick_glu_silu_srt_e_kernel(tc, xT, w1, w3, w2, offs, out):
         up(0, 4)
         quantize("w3_1")
         quantize_h(0, 0, 512)
-        cast("w2_0", (("S", 32), ("S", 32)))
-        gate(0, 5)
-        gate(1, 4)
-        gate(1, 5)
+        cast("w2_0", (("S", 64),))
+        for s in range(5, 8):
+            gate(0, s)
         for s in range(4):
             up(1, s)
         cast("w2_1", (("S", 48), ("V", 16)))
         quantize("w2_0")
         quantize_h(1, 0, 512)
         quantize("w2_1")
-        gate(0, 6)
-        gate(0, 7)
-        gate(1, 6)
-        gate(1, 7)
+        for s in range(4, 8):
+            gate(1, s, over="w2_1")
         up(0, 5, "y")
         up(1, 4)
         up(1, 5)
@@ -334,15 +339,18 @@ def tile_picked_pick_glu_silu_srt_e_kernel(tc, xT, w1, w3, w2, offs, out):
         up_product(1, 7)
         quantize_h(0, 512, 768)
         for m in range(4):
-            output((m,), 0, 512, "gate", "SSSS"[m])
+            output((m,), 0, 512, "gate", "SSSS"[m], (0, 1))
         up(0, 6)
         quantize_h(1, 512, 768)
         up(0, 7)
-        up(1, 6)
-        quantize_h(0, 768, 1024)
         output((0, 1), 512, 768, "y", "S")
         output((2, 3), 512, 768, "gate", "S")
+        up(1, 6)
+        quantize_h(0, 768, 1024)
+        quantize_h(1, 768, 896)
         up(1, 7)
-        open_output(768, 1024, ("gate", "y", "up", "up"))
-        quantize_h(1, 768, 1024)
-        close_output(768, 1024, "VSVS")
+        output((0, 1), 768, 896, "gate", "V")
+        output((2, 3), 768, 896, "y", "S")
+        open_output(896, 1024, ("up", "up", "gate", "y"))
+        quantize_h(1, 896, 1024)
+        close_in_pairs(896, 1024)

@@ -17,40 +17,49 @@ MULT = mybir.AluOpType.mult
 P = 128
 PACK = 4
 PASS = P * PACK
-SLICE = 128
+UNIT = 128
+HALF = S // 2
+QUARTER = S // 4
+LIST_ROWS = 16
 FLOPS = 2 * S * (2 * K * H + H * N)
+
+TOKEN_CUTS = (0, 1024, 1536, 2048)
+LOAD_ORDER = ("x0", "offs", "x1", "x2", "w1_0", "w3_0", "w1_1", "w3_1", "w2_0", "w2_1")
+BANKS = {"gate": 3, "up": 3, "spare": 2}
+SILU_TILES = 8
+W2_SCALAR_COLUMNS = 384
 
 
 def tile_picked_pick_glu_silu_srt_e_kernel(tc, xT, w1, w3, w2, offs, out):
     nc = tc.nc
     with ExitStack() as ctx:
         keep = ctx.enter_context(tc.tile_pool(name="keep", bufs=1))
-        ring = ctx.enter_context(tc.tile_pool(name="ring", bufs=12))
+        ring = ctx.enter_context(tc.tile_pool(name="ring", bufs=SILU_TILES))
         acc = ctx.enter_context(tc.psum_pool(name="acc", bufs=3))
 
-        offsets = keep.tile([P, S // 16], U16, name="offsets")
-        warm = keep.tile([P, 1], F32, name="warm")
-        nc.vector.memset(warm[:], 0.0)
-        nc.scalar.activation(warm[:], warm[:], SILU)
-        all_bytes = keep.tile([P, T], U8, name="all_bytes", align_bytes=64)
-        nc.gpsimd.memset(all_bytes[:], 0)
-        all_words = keep.tile([P, T], U32, name="all_words", align_bytes=64)
+        offsets = keep.tile([P, S // LIST_ROWS], U16, name="offsets")
+        table_load = keep.tile([P, 1], F32, name="table_load")
+        nc.vector.memset(table_load[:], 0.0)
+        nc.scalar.activation(table_load[:], table_load[:], SILU)
+        token_bytes = keep.tile([P, T], U8, name="token_bytes", align_bytes=64)
+        nc.gpsimd.memset(token_bytes[:], 0)
+        token_words = keep.tile([P, T], U32, name="token_words", align_bytes=64)
 
         sources = {}
-        token_cuts = (0, 1024, 1536, 2048)
-        for c in range(len(token_cuts) - 1):
-            sources["x%d" % c] = xT[:, token_cuts[c] : token_cuts[c + 1]]
+        for c in range(len(TOKEN_CUTS) - 1):
+            sources["x%d" % c] = xT[:, TOKEN_CUTS[c] : TOKEN_CUTS[c + 1]]
         for g in range(2):
-            sources["w1_%d" % g] = w1[:, g * 512 : (g + 1) * 512]
-            sources["w3_%d" % g] = w3[:, g * 512 : (g + 1) * 512]
-            sources["w2_%d" % g] = w2[g * 512 : (g + 1) * 512, :]
+            sources["w1_%d" % g] = w1[:, g * PASS : (g + 1) * PASS]
+            sources["w3_%d" % g] = w3[:, g * PASS : (g + 1) * PASS]
+            sources["w2_%d" % g] = w2[g * PASS : (g + 1) * PASS, :]
+
         raw = {}
-        for name in ["x0","offs","x1","x2","w1_0","w3_0","w1_1","w3_1","w2_0","w2_1"]:
+        for name in LOAD_ORDER:
             if name == "offs":
                 nc.sync.dma_start(offsets[:], offs)
             else:
                 tile = keep.tile([P, PACK, sources[name].shape[1]], F32, name="raw_" + name, tag="raw_" + name, align_bytes=64)
-                if name[:2] == "w2":
+                if name.startswith("w2"):
                     dealt = sources[name].rearrange("(q t e) c -> t q e c", t=PACK, e=2)
                     for t in range(PACK):
                         nc.sync.dma_start(out=tile[:, t, :], in_=dealt[t])
@@ -58,299 +67,226 @@ def tile_picked_pick_glu_silu_srt_e_kernel(tc, xT, w1, w3, w2, offs, out):
                     nc.sync.dma_start(out=tile[:], in_=sources[name].rearrange("(p j) c -> p j c", j=PACK))
                 raw[name] = tile[:]
 
-        grouped = {}
+        rounded = {}
         codes = {}
         scales = {}
 
-        def cast(name, shares, start=0):
-            if start == 0:
-                fresh = keep.tile([P, PACK * sources[name].shape[1]], BF16, name="grouped_" + name, align_bytes=64)
-                grouped[name] = fresh
-            tile = grouped[name]
-            if name[:2] in ("w1", "w3"):
-                dst = tile[:].rearrange("p (t q e j) -> p q t j e", t=PACK, e=2, j=PACK)
-                src = raw[name].rearrange("p j (q t e) -> p q t j e", t=PACK, e=2)
-            else:
-                dst = tile[:].rearrange("p (q t e j) -> p q t j e", t=PACK, e=2, j=PACK)
-                src = raw[name].rearrange("p j (q t e) -> p q t j e", t=PACK, e=2)
-            for engine, count in shares:
-                part = slice(start, start + count)
-                if engine == "V":
-                    nc.vector.tensor_copy(out=dst[:, part], in_=src[:, part])
-                elif name[0] == "x":
-                    nc.scalar.activation(dst[:, part], src[:, part], COPY)
-                else:
-                    nc.scalar.copy(dst[:, part], src[:, part])
-                start = start + count
+        def rounded_tile(name):
+            if name not in rounded:
+                tile = keep.tile([P, PACK * sources[name].shape[1]], BF16, name="rounded_" + name, align_bytes=64)
+                rounded[name] = tile
+            return rounded[name][:]
 
-        def cast_slots(name, engine, first, last):
-            if name not in grouped:
-                fresh = keep.tile([P, PACK * 512], BF16, name="grouped_" + name, align_bytes=64)
-                grouped[name] = fresh
-            dst = grouped[name][:].rearrange("p (t q e j) -> p q t j e", t=PACK, e=2, j=PACK)[:, :, first:last]
-            src = raw[name].rearrange("p j (q t e) -> p q t j e", t=PACK, e=2)[:, :, first:last]
+        def move(engine, name, dst, src):
             if engine == "V":
                 nc.vector.tensor_copy(out=dst, in_=src)
+            elif name.startswith("x"):
+                nc.scalar.activation(dst, src, COPY)
             else:
                 nc.scalar.copy(dst, src)
 
-        def cast_on_gpsimd(name, pieces):
-            fresh = keep.tile([P, PACK * 512], BF16, name="grouped_" + name, align_bytes=64)
-            grouped[name] = fresh
-            dst = fresh[:].rearrange("p (c j) -> p c j", j=PACK)
-            src = raw[name].rearrange("p j c -> p c j")
-            width = 512 // pieces
-            for piece in range(pieces):
-                part = slice(piece * width, (piece + 1) * width)
-                nc.gpsimd.tensor_scalar(
-                    out=dst[:, part], in0=src[:, part], scalar1=1.0, scalar2=0.0, op0=MULT, op1=mybir.AluOpType.add
-                )
+        def cast_columns(name, engine, first, last):
+            runs = slice(first // 8, last // 8)
+            dst = rounded_tile(name).rearrange("p (q t e j) -> p q t j e", t=PACK, e=2, j=PACK)
+            src = raw[name].rearrange("p j (q t e) -> p q t j e", t=PACK, e=2)
+            move(engine, name, dst[:, runs], src[:, runs])
 
-        def quantize_part(name, first, last):
-            values = grouped[name][:, first * PACK : last * PACK]
-            if name[0] == "x":
-                base = token_cuts[int(name[1:])]
-                cols = slice(base + first, base + last)
-                nc.vector.quantize_mx(out=all_words[:, cols].bitcast(FP8X4), scales=all_bytes[:, cols], in_=values)
-            else:
-                if name not in codes:
-                    code = keep.tile([P, 512], U32, name="codes_" + name, align_bytes=64)
-                    scale = keep.tile([P, 512], U8, name="scales_" + name, align_bytes=64)
-                    codes[name] = code
-                    scales[name] = scale
-                nc.vector.quantize_mx(out=codes[name][:, first:last].bitcast(FP8X4), scales=scales[name][:, first:last], in_=values)
+        def cast_slots(name, engine, first, last):
+            dst = rounded_tile(name).rearrange("p (t q e j) -> p q t j e", t=PACK, e=2, j=PACK)
+            src = raw[name].rearrange("p j (q t e) -> p q t j e", t=PACK, e=2)
+            move(engine, name, dst[:, :, first:last], src[:, :, first:last])
 
-        def quantize(name):
-            if name[0] == "x":
-                cols = slice(token_cuts[int(name[1:])], token_cuts[int(name[1:]) + 1])
-                nc.vector.quantize_mx(out=all_words[:, cols].bitcast(FP8X4), scales=all_bytes[:, cols], in_=grouped[name][:])
-            else:
-                code = keep.tile([P, 512], U32, name="codes_" + name, align_bytes=64)
-                scale = keep.tile([P, 512], U8, name="scales_" + name, align_bytes=64)
-                nc.vector.quantize_mx(out=code[:].bitcast(FP8X4), scales=scale[:], in_=grouped[name][:])
-                codes[name] = code
-                scales[name] = scale
+        def quantize(words, plane, values):
+            nc.vector.quantize_mx(out=words.bitcast(FP8X4), scales=plane, in_=values)
+
+        def quantize_tokens(c, first, last):
+            cols = slice(TOKEN_CUTS[c] + first, TOKEN_CUTS[c] + last)
+            quantize(token_words[:, cols], token_bytes[:, cols], rounded["x%d" % c][:, first * PACK : last * PACK])
+
+        def quantize_weights(name, first, last):
+            if name not in codes:
+                words = keep.tile([P, PASS], U32, name="codes_" + name, align_bytes=64)
+                plane = keep.tile([P, PASS], U8, name="scales_" + name, align_bytes=64)
+                codes[name] = words
+                scales[name] = plane
+            quantize(codes[name][:, first:last], scales[name][:, first:last], rounded[name][:, first * PACK : last * PACK])
 
         picked_words = keep.tile([P, S], U32, name="picked_words", align_bytes=64)
-        early_bytes = keep.tile([P, S // 2], U8, name="early_bytes", align_bytes=64)
-        late_bytes = keep.tile([P, S // 2], U8, name="late_bytes", tag="raw_w1_0", align_bytes=64)
+        early_bytes = keep.tile([P, HALF], U8, name="early_bytes", align_bytes=64)
+        late_bytes = keep.tile([P, HALF], U8, name="late_bytes", tag="raw_w1_0", align_bytes=64)
         picked_bytes = (early_bytes, late_bytes)
 
-        def gather(picked, window, first, last):
-            reach = last + T - S
-            entries = offsets[:, first // 16 : last // 16]
-            if window is all_bytes:
-                dst = picked[first // 512][:]
-            else:
-                dst = picked[:, first:last]
-            nc.vector.tensor_copy(out=dst, in_=window[:, 0:reach].indirect(entries))
+        def gather(dst, window, half):
+            first, last = half * HALF, (half + 1) * HALF
+            entries = offsets[:, first // LIST_ROWS : last // LIST_ROWS]
+            nc.vector.tensor_copy(out=dst, in_=window[:, 0 : last + T - S].indirect(entries))
 
-        H_OVER = ("raw_w1_1", "h_second")
-        h_grouped = []
+        h_tags = ("raw_w1_1", "h_rounded1")
+        h_rounded = []
         h_codes = []
         h_scales = []
         for g in range(2):
-            a = keep.tile([P, S, PACK], BF16, name="h_grouped%d" % g, tag=H_OVER[g], align_bytes=64)
-            b = keep.tile([P, S], U32, name="h_codes%d" % g, align_bytes=64)
-            c = keep.tile([P, S], U8, name="h_scales%d" % g, align_bytes=64)
-            h_grouped.append(a)
-            h_codes.append(b)
-            h_scales.append(c)
+            values = keep.tile([P, S, PACK], BF16, name="h_rounded%d" % g, tag=h_tags[g], align_bytes=64)
+            words = keep.tile([P, S], U32, name="h_codes%d" % g, align_bytes=64)
+            plane = keep.tile([P, S], U8, name="h_scales%d" % g, align_bytes=64)
+            h_rounded.append(values)
+            h_codes.append(words)
+            h_scales.append(plane)
 
-        acts = {}
-
-        def hidden(layer, g, s, tag):
-            cols = slice(s * SLICE, (s + 1) * SLICE)
-            bank = acc.tile([P, PACK, SLICE], F32, name=tag, tag=tag, bufs=2 if tag == "y" else 3)
-            for t in range(PACK):
-                rows = slice(t * P, (t + 1) * P)
-                nc.tensor.matmul_mx(
-                    out=bank[:, t, :],
-                    lhsT=codes[layer % g][:, rows].bitcast(FP8X4),
-                    lhsT_scale=scales[layer % g][:, rows],
-                    rhs=picked_words[:, cols].bitcast(FP8X4),
-                    rhs_scale=picked_bytes[s // 4][:, (s % 4) * SLICE : (s % 4 + 1) * SLICE],
-                    start=True,
-                    stop=True,
-                )
-            return bank[:].rearrange("p t n -> p n t")
-
-        reused = {}
-
-        def gate(g, s, over=None):
-            bank = hidden("w1_%d", g, s, "gate")
-            if over is None:
-                fresh = ring.tile([P, SLICE, PACK], F32, name="act")
-                act = fresh[:]
-            else:
-                if over not in reused:
-                    four = keep.tile([P, PACK, SLICE, PACK], F32, name="acts_" + over, tag="raw_" + over, align_bytes=64)
-                    reused[over] = four
-                act = reused[over][:, s % PACK]
-            nc.scalar.activation(act, bank, SILU)
-            acts[g, s] = act
-
-        up_banks = {}
-
-        def up_product(g, s, tag="up"):
-            up_banks[g, s] = hidden("w3_%d", g, s, tag)
-
-        def up(g, s, tag="up"):
-            if (g, s) not in up_banks:
-                up_product(g, s, tag)
-            bank = up_banks[g, s]
-            nc.vector.tensor_tensor(out=h_grouped[g][:, s * SLICE : (s + 1) * SLICE, :], in0=bank, in1=acts[g, s], op=MULT)
-
-        def warm_tensor(passes):
-            idle = acc.tile([P, 512], F32, name="idle", tag="y", bufs=2)
-            for turn in range(passes):
-                nc.tensor.matmul_mx(
-                    out=idle[:],
-                    lhsT=picked_words[:, 512:640].bitcast(FP8X4),
-                    lhsT_scale=early_bytes[:, 0:128],
-                    rhs=picked_words[:, 0:512].bitcast(FP8X4),
-                    rhs_scale=early_bytes[:],
-                    start=True,
-                    stop=True,
-                )
-
-        def quantize_h(g, first, last):
-            nc.vector.quantize_mx(
-                out=h_codes[g][:, first:last].bitcast(FP8X4),
-                scales=h_scales[g][:, first:last],
-                in_=h_grouped[g][:, first:last, :].rearrange("p n t -> p (n t)"),
-            )
-
-        y_banks = {}
-
-        def bank_tile(width, name, tag):
-            return acc.tile([P, width], F32, name=name, tag=tag, bufs=2 if tag == "y" else 3)
-
-        def one_pass(dst, m, first, last, g, opens):
-            rows = slice(m * P, (m + 1) * P)
+        def multiply(dst, name, rows, words, plane, start, stop):
             nc.tensor.matmul_mx(
                 out=dst,
-                lhsT=codes["w2_%d" % g][:, rows].bitcast(FP8X4),
-                lhsT_scale=scales["w2_%d" % g][:, rows],
-                rhs=h_codes[g][:, first:last].bitcast(FP8X4),
-                rhs_scale=h_scales[g][:, first:last],
-                start=opens,
-                stop=not opens,
+                lhsT=codes[name][:, rows].bitcast(FP8X4),
+                lhsT_scale=scales[name][:, rows],
+                rhs=words.bitcast(FP8X4),
+                rhs_scale=plane,
+                start=start,
+                stop=stop,
             )
 
-        def leave(bank, blocks, first, last, engine):
-            width = last - first
-            y = keep.tile([P, len(blocks), width], F32, name="y_out%d_%d" % (first, blocks[0]))
-            flat = y[:].rearrange("p m n -> p (m n)")
-            if engine == "S":
-                nc.scalar.copy(flat, bank[:])
+        def unit_products(name, u, kind):
+            bank = acc.tile([P, PACK, UNIT], F32, name=kind, tag=kind, bufs=BANKS[kind])
+            half, place = divmod(u * UNIT, HALF)
+            words = picked_words[:, u * UNIT : (u + 1) * UNIT]
+            plane = picked_bytes[half][:, place : place + UNIT]
+            for t in range(PACK):
+                multiply(bank[:, t, :], name, slice(t * P, (t + 1) * P), words, plane, True, True)
+            return bank[:].rearrange("p t n -> p n t")
+
+        silus = {}
+        silu_quads = {}
+        up_banks = {}
+
+        def gate(g, u, over=None):
+            bank = unit_products("w1_%d" % g, u, "gate")
+            if over is None:
+                tile = ring.tile([P, UNIT, PACK], F32, name="silu")
+                values = tile[:]
             else:
-                nc.vector.tensor_copy(out=flat, in_=bank[:])
-            rows = out[blocks[0] * P : (blocks[-1] + 1) * P, first:last]
-            nc.sync.dma_start(out=rows.rearrange("(m p) n -> p m n", p=P), in_=y[:])
+                if over not in silu_quads:
+                    quad = keep.tile([P, PACK, UNIT, PACK], F32, name="silus_" + over, tag="raw_" + over, align_bytes=64)
+                    silu_quads[over] = quad
+                values = silu_quads[over][:, u % PACK]
+            nc.scalar.activation(values, bank, SILU)
+            silus[g, u] = values
 
-        def output(blocks, first, last, tag, engine, groups=(1, 0)):
+        def up(g, u, kind="up"):
+            up_banks[g, u] = unit_products("w3_%d" % g, u, kind)
+
+        def gated(g, u):
+            dst = h_rounded[g][:, u * UNIT : (u + 1) * UNIT, :]
+            nc.vector.tensor_tensor(out=dst, in0=up_banks[g, u], in1=silus[g, u], op=MULT)
+
+        def up_and_gated(g, u, kind="up"):
+            up(g, u, kind)
+            gated(g, u)
+
+        def quantize_h(g, first, last):
+            values = h_rounded[g][:, first:last, :].rearrange("p n t -> p (n t)")
+            quantize(h_codes[g][:, first:last], h_scales[g][:, first:last], values)
+
+        def output_pass(dst, m, first, last, g, opens):
+            words, plane = h_codes[g][:, first:last], h_scales[g][:, first:last]
+            multiply(dst, "w2_%d" % g, slice(m * P, (m + 1) * P), words, plane, opens, not opens)
+
+        def store(values, m, blocks, first, last):
+            rows = out[m * P : (m + blocks) * P, first:last]
+            nc.sync.dma_start(out=rows.rearrange("(m p) n -> p m n", p=P), in_=values)
+
+        def output(m, blocks, first, last, kind, groups):
             width = last - first
-            bank = bank_tile(len(blocks) * width, "y%d_%d" % (first, blocks[0]), tag)
-            for place, m in enumerate(blocks):
+            bank = acc.tile([P, blocks * width], F32, name="y_bank", tag=kind, bufs=BANKS[kind])
+            for place in range(blocks):
                 for g in groups:
-                    one_pass(bank[:, place * width : (place + 1) * width], m, first, last, g, g == groups[0])
-            leave(bank, blocks, first, last, engine)
+                    output_pass(bank[:, place * width : (place + 1) * width], m + place, first, last, g, g == groups[0])
+            y = keep.tile([P, blocks, width], F32, name="y%d_%d" % (first, m))
+            nc.scalar.copy(y[:].rearrange("p m n -> p (m n)"), bank[:])
+            store(y[:], m, blocks, first, last)
 
-        def open_output(first, last, tags):
-            for m, tag in enumerate(tags):
-                bank = bank_tile(last - first, "y%d_%d" % (first, m), tag)
-                y_banks[first, m] = bank
-                one_pass(bank[:], m, first, last, 0, True)
+        cast_columns("x0", "V", 0, 512)
+        cast_columns("x0", "S", 512, 1024)
+        quantize_tokens(0, 0, 512)
+        quantize_tokens(0, 512, 1024)
+        cast_columns("x1", "S", 0, 256)
+        cast_columns("x1", "V", 256, 512)
+        quantize_tokens(1, 0, 256)
+        quantize_tokens(1, 256, 512)
+        gather(picked_words[:, 0:HALF], token_words, 0)
+        gather(early_bytes[:], token_bytes, 0)
+        cast_columns("x2", "S", 0, 256)
+        cast_columns("x2", "S", 256, 512)
+        quantize_tokens(2, 0, 256)
+        quantize_tokens(2, 256, 512)
 
-        def close_in_pairs(first, last):
-            width = last - first
-            for pair in range(2):
-                y = keep.tile([P, 2, width], F32, name="y_last%d" % pair)
-                for place in range(2):
-                    m = 2 * pair + place
-                    one_pass(y_banks[first, m][:], m, first, last, 1, False)
-                    if place == 0:
-                        nc.scalar.copy(y[:, place, :], y_banks[first, m][:])
-                    else:
-                        nc.vector.tensor_copy(out=y[:, place, :], in_=y_banks[first, m][:])
-                rows = out[2 * pair * P : (2 * pair + 2) * P, first:last]
-                nc.sync.dma_start(out=rows.rearrange("(m p) n -> p m n", p=P), in_=y[:])
-
-        def close_output(first, last, engines):
-            for m, engine in enumerate(engines):
-                one_pass(y_banks[first, m][:], m, first, last, 1, False)
-                leave(y_banks[first, m], (m,), first, last, engine)
-
-        cast("x0", (("V", 64), ("S", 64)))
-        quantize_part("x0", 0, 512)
-        quantize_part("x0", 512, 1024)
-        cast("x1", (("S", 32), ("V", 32)))
-        quantize_part("x1", 0, 256)
-        quantize_part("x1", 256, 512)
-        gather(picked_words, all_words, 0, 512)
-        gather(picked_bytes, all_bytes, 0, 512)
-        cast("x2", (("S", 32), ("S", 32)))
-        quantize_part("x2", 0, 256)
-        quantize_part("x2", 256, 512)
         cast_slots("w1_0", "S", 0, 2)
         cast_slots("w1_0", "S", 2, 3)
-        gather(picked_words, all_words, 512, 1024)
+        gather(picked_words[:, HALF:S], token_words, 1)
         cast_slots("w1_0", "V", 3, 4)
-        quantize_part("w1_0", 0, 256)
-        quantize_part("w1_0", 256, 512)
-        gather(picked_bytes, all_bytes, 512, 1024)
+        quantize_weights("w1_0", 0, 256)
+        quantize_weights("w1_0", 256, 512)
+        gather(late_bytes[:], token_bytes, 1)
         cast_slots("w3_0", "S", 0, 2)
         cast_slots("w3_0", "V", 3, 4)
         cast_slots("w3_0", "S", 2, 3)
-        quantize_part("w3_0", 0, 256)
-        quantize_part("w3_0", 256, 512)
-        for s in range(4):
-            gate(0, s, over="w3_0")
+        quantize_weights("w3_0", 0, 256)
+        quantize_weights("w3_0", 256, 512)
+
+        for u in range(4):
+            gate(0, u, over="w3_0")
         gate(0, 4)
-        cast("w1_1", (("V", 64),))
-        up(0, 0)
-        quantize("w1_1")
-        for s in range(4):
-            gate(1, s)
-        for s in range(1, 4):
-            up(0, s)
-        cast("w3_1", (("V", 64),))
-        up(0, 4)
-        quantize("w3_1")
-        quantize_h(0, 0, 512)
-        cast("w2_0", (("S", 64),))
-        for s in range(5, 8):
-            gate(0, s)
-        for s in range(4):
-            up(1, s)
-        cast("w2_1", (("S", 48), ("V", 16)))
-        quantize("w2_0")
-        quantize_h(1, 0, 512)
-        quantize("w2_1")
-        for s in range(4, 8):
-            gate(1, s, over="w2_1")
-        up(0, 5, "y")
-        up(1, 4)
-        up(1, 5)
-        up_product(0, 6, "y")
-        up_product(0, 7, "y")
-        up_product(1, 6)
-        up_product(1, 7)
-        quantize_h(0, 512, 768)
-        for m in range(4):
-            output((m,), 0, 512, "gate", "SSSS"[m], (0, 1))
-        up(0, 6)
-        quantize_h(1, 512, 768)
-        up(0, 7)
-        output((0, 1), 512, 768, "y", "S")
-        output((2, 3), 512, 768, "gate", "S")
+        cast_slots("w1_1", "V", 0, PACK)
+        up_and_gated(0, 0)
+        quantize_weights("w1_1", 0, PASS)
+        for u in range(4):
+            gate(1, u)
+        for u in range(1, 4):
+            up_and_gated(0, u)
+        cast_slots("w3_1", "V", 0, PACK)
+        up_and_gated(0, 4)
+        quantize_weights("w3_1", 0, PASS)
+        quantize_h(0, 0, HALF)
+        cast_columns("w2_0", "S", 0, N)
+        for u in range(5, 8):
+            gate(0, u)
+        for u in range(4):
+            up_and_gated(1, u)
+        cast_columns("w2_1", "S", 0, W2_SCALAR_COLUMNS)
+        cast_columns("w2_1", "V", W2_SCALAR_COLUMNS, N)
+        quantize_weights("w2_0", 0, N)
+        quantize_h(1, 0, HALF)
+        quantize_weights("w2_1", 0, N)
+
+        for u in range(4, 8):
+            gate(1, u, over="w2_1")
+        up_and_gated(0, 5, "spare")
+        up_and_gated(1, 4)
+        up_and_gated(1, 5)
+        up(0, 6, "spare")
+        up(0, 7, "spare")
         up(1, 6)
-        quantize_h(0, 768, 1024)
-        quantize_h(1, 768, 896)
         up(1, 7)
-        output((0, 1), 768, 896, "gate", "V")
-        output((2, 3), 768, 896, "y", "S")
-        open_output(896, 1024, ("up", "up", "gate", "y"))
-        quantize_h(1, 896, 1024)
-        close_in_pairs(896, 1024)
+        quantize_h(0, HALF, HALF + QUARTER)
+        for m in range(4):
+            output(m, 1, 0, HALF, "gate", (0, 1))
+        gated(0, 6)
+        quantize_h(1, HALF, HALF + QUARTER)
+        gated(0, 7)
+        output(0, 2, HALF, HALF + QUARTER, "spare", (1, 0))
+        output(2, 2, HALF, HALF + QUARTER, "gate", (1, 0))
+        gated(1, 6)
+        quantize_h(0, S - QUARTER, S)
+        gated(1, 7)
+
+        last_banks = []
+        for m, kind in enumerate(("gate", "spare", "up", "up")):
+            bank = acc.tile([P, QUARTER], F32, name="y_bank", tag=kind, bufs=BANKS[kind])
+            last_banks.append(bank)
+            output_pass(bank[:], m, S - QUARTER, S, 0, True)
+        quantize_h(1, S - QUARTER, S)
+        for m in (0, 2):
+            y = keep.tile([P, 2, QUARTER], F32, name="y_last%d" % m)
+            output_pass(last_banks[m][:], m, S - QUARTER, S, 1, False)
+            nc.scalar.copy(y[:, 0, :], last_banks[m][:])
+            output_pass(last_banks[m + 1][:], m + 1, S - QUARTER, S, 1, False)
+            nc.vector.tensor_copy(out=y[:, 1, :], in_=last_banks[m + 1][:])
+            store(y[:], m, 2, S - QUARTER, S)

@@ -26,7 +26,7 @@ FLOPS = 2 * S * (2 * K * H + H * N)
 TOKEN_CUTS = (0, 1024, 1536, 2048)
 LOAD_ORDER = ("x0", "offs", "x1", "x2", "w1_0", "w3_0", "w1_1", "w3_1", "w2_0", "w2_1")
 BANKS = {"gate": 3, "up": 3, "spare": 2}
-SILU_TILES = 8
+SILU_TILES = 4
 W2_SCALAR_COLUMNS = 384
 
 
@@ -157,25 +157,33 @@ def tile_picked_pick_glu_silu_srt_e_kernel(tc, xT, w1, w3, w2, offs, out):
         silu_quads = {}
         up_banks = {}
 
-        def gate(g, u, over=None):
-            bank = unit_products("w1_%d" % g, u, "gate")
+        def gate(g, v, over=None):
             if over is None:
-                tile = ring.tile([P, UNIT, PACK], F32, name="silu")
+                tile = ring.tile([P, 2, 2 * UNIT, 2], F32, name="silu")
                 values = tile[:]
             else:
                 if over not in silu_quads:
-                    quad = keep.tile([P, PACK, UNIT, PACK], F32, name="silus_" + over, tag="raw_" + over, align_bytes=64)
+                    quad = keep.tile([P, 2, 2, 2 * UNIT, 2], F32, name="silus_" + over, tag="raw_" + over, align_bytes=64)
                     silu_quads[over] = quad
-                values = silu_quads[over][:, u % PACK]
-            nc.scalar.activation(values, bank, SILU)
-            silus[g, u] = values
+                values = silu_quads[over][:, v % 2]
+            half, place = divmod(2 * v * UNIT, HALF)
+            words = picked_words[:, 2 * v * UNIT : (2 * v + 2) * UNIT]
+            plane = picked_bytes[half][:, place : place + 2 * UNIT]
+            for pair in range(2):
+                bank = acc.tile([P, 2, 2 * UNIT], F32, name="gate", tag="gate", bufs=BANKS["gate"])
+                for s in range(2):
+                    t = 2 * pair + s
+                    multiply(bank[:, s, :], "w1_%d" % g, slice(t * P, (t + 1) * P), words, plane, True, True)
+                nc.scalar.activation(values[:, pair], bank[:].rearrange("p s n -> p n s"), SILU)
+            for r in range(2):
+                silus[g, 2 * v + r] = values[:, :, r * UNIT : (r + 1) * UNIT, :].rearrange("p a n s -> p n a s")
 
         def up(g, u, kind="up"):
             up_banks[g, u] = unit_products("w3_%d" % g, u, kind)
 
         def gated(g, u):
-            dst = h_rounded[g][:, u * UNIT : (u + 1) * UNIT, :]
-            nc.vector.tensor_tensor(out=dst, in0=up_banks[g, u], in1=silus[g, u], op=MULT)
+            dst = h_rounded[g][:, u * UNIT : (u + 1) * UNIT, :].rearrange("p n (a s) -> p n a s", a=2)
+            nc.vector.tensor_tensor(out=dst, in0=up_banks[g, u].rearrange("p n (a s) -> p n a s", a=2), in1=silus[g, u], op=MULT)
 
         def up_and_gated(g, u, kind="up"):
             up(g, u, kind)
@@ -231,14 +239,14 @@ def tile_picked_pick_glu_silu_srt_e_kernel(tc, xT, w1, w3, w2, offs, out):
         quantize_weights("w3_0", 0, 256)
         quantize_weights("w3_0", 256, 512)
 
-        for u in range(4):
-            gate(0, u, over="w3_0")
-        gate(0, 4)
+        for v in range(2):
+            gate(0, v, over="w3_0")
+        gate(0, 2)
         cast_slots("w1_1", "V", 0, PACK)
         up_and_gated(0, 0)
         quantize_weights("w1_1", 0, PASS)
-        for u in range(4):
-            gate(1, u)
+        for v in range(2):
+            gate(1, v)
         for u in range(1, 4):
             up_and_gated(0, u)
         cast_slots("w3_1", "V", 0, PACK)
@@ -246,8 +254,7 @@ def tile_picked_pick_glu_silu_srt_e_kernel(tc, xT, w1, w3, w2, offs, out):
         quantize_weights("w3_1", 0, PASS)
         quantize_h(0, 0, HALF)
         cast_columns("w2_0", "S", 0, N)
-        for u in range(5, 8):
-            gate(0, u)
+        gate(0, 3)
         for u in range(4):
             up_and_gated(1, u)
         cast_columns("w2_1", "S", 0, W2_SCALAR_COLUMNS)
@@ -256,37 +263,74 @@ def tile_picked_pick_glu_silu_srt_e_kernel(tc, xT, w1, w3, w2, offs, out):
         quantize_h(1, 0, HALF)
         quantize_weights("w2_1", 0, N)
 
-        for u in range(4, 8):
-            gate(1, u, over="w2_1")
+        for v in range(2, 4):
+            gate(1, v, over="w2_1")
         up_and_gated(0, 5, "spare")
-        up_and_gated(1, 4)
-        up_and_gated(1, 5)
+        up(1, 4)
+        up(1, 5)
         up(0, 6, "spare")
         up(0, 7, "spare")
+        banks = {}
+
+        def open_sum(m, blocks, first, last, kind, g):
+            width = last - first
+            bank = acc.tile([P, blocks * width], F32, name="y_bank", tag=kind, bufs=BANKS[kind])
+            banks[m, first] = bank
+            for place in range(blocks):
+                words, plane = h_codes[g][:, first:last], h_scales[g][:, first:last]
+                multiply(bank[:, place * width : (place + 1) * width], "w2_%d" % g, slice((m + place) * P, (m + place + 1) * P), words, plane, place == 0, False)
+
+        def close_sum(m, blocks, first, last, g, engine):
+            width = last - first
+            bank = banks[m, first]
+            for place in range(blocks):
+                words, plane = h_codes[g][:, first:last], h_scales[g][:, first:last]
+                multiply(bank[:, place * width : (place + 1) * width], "w2_%d" % g, slice((m + place) * P, (m + place + 1) * P), words, plane, False, place == blocks - 1)
+            y = keep.tile([P, blocks, width], F32, name="y%d_%d" % (first, m))
+            move(engine, "y", y[:].rearrange("p m n -> p (m n)"), bank[:])
+            store(y[:], m, blocks, first, last)
+
+        open_sum(0, 1, 0, HALF, "up", 0)
+        close_sum(0, 1, 0, HALF, 1, "S")
+
+        gated(1, 4)
         up(1, 6)
+        gated(1, 5)
         up(1, 7)
         quantize_h(0, HALF, HALF + QUARTER)
-        for m in range(4):
-            output(m, 1, 0, HALF, "gate", (0, 1))
+        for m in range(1, 4):
+            open_sum(m, 1, 0, HALF, "gate", 0)
+            close_sum(m, 1, 0, HALF, 1, "S")
         gated(0, 6)
         quantize_h(1, HALF, HALF + QUARTER)
         gated(0, 7)
-        output(0, 2, HALF, HALF + QUARTER, "spare", (1, 0))
-        output(2, 2, HALF, HALF + QUARTER, "gate", (1, 0))
+        for m in (0, 2):
+            open_sum(m, 2, HALF, HALF + QUARTER, "spare", 0)
+        for m in (0, 2):
+            close_sum(m, 2, HALF, HALF + QUARTER, 1, "S")
         gated(1, 6)
         quantize_h(0, S - QUARTER, S)
+        quantize_h(1, S - QUARTER, S - UNIT)
         gated(1, 7)
 
+        def shared_passes(bank, m, blocks, u, g):
+            cols = slice(u * UNIT, (u + 1) * UNIT)
+            for place in range(blocks):
+                rows = slice((m + place) * P, (m + place + 1) * P)
+                opens, closes = g == 0 and place == 0, g == 1 and place == blocks - 1
+                multiply(bank[:, place, :], "w2_%d" % g, rows, h_codes[g][:, cols], h_scales[g][:, cols], opens, closes)
+
+        pieces = ((6, 0, 4, "up", "S"), (7, 0, 2, "gate", "V"), (7, 2, 2, "gate", "S"))
         last_banks = []
-        for m, kind in enumerate(("gate", "spare", "up", "up")):
-            bank = acc.tile([P, QUARTER], F32, name="y_bank", tag=kind, bufs=BANKS[kind])
+        for u, m, blocks, kind, engine in pieces:
+            bank = acc.tile([P, blocks, UNIT], F32, name="y_bank", tag=kind, bufs=BANKS[kind])
             last_banks.append(bank)
-            output_pass(bank[:], m, S - QUARTER, S, 0, True)
-        quantize_h(1, S - QUARTER, S)
+            shared_passes(bank, m, blocks, u, 0)
+        quantize_h(1, S - UNIT, S)
+        y = keep.tile([P, PACK, QUARTER], F32, name="y_last")
+        for bank, (u, m, blocks, kind, engine) in zip(last_banks, pieces):
+            shared_passes(bank, m, blocks, u, 1)
+            first = u * UNIT - (S - QUARTER)
+            move(engine, "y", y[:, m : m + blocks, first : first + UNIT], bank[:])
         for m in (0, 2):
-            y = keep.tile([P, 2, QUARTER], F32, name="y_last%d" % m)
-            output_pass(last_banks[m][:], m, S - QUARTER, S, 1, False)
-            nc.scalar.copy(y[:, 0, :], last_banks[m][:])
-            output_pass(last_banks[m + 1][:], m + 1, S - QUARTER, S, 1, False)
-            nc.vector.tensor_copy(out=y[:, 1, :], in_=last_banks[m + 1][:])
-            store(y[:], m, 2, S - QUARTER, S)
+            store(y[:, m : m + 2, :], m, 2, S - QUARTER, S)

@@ -89,12 +89,22 @@ def tile_picked_pick_glu_silu_srt_e_kernel(tc, xT, w1, w3, w2, offs, out):
             runs = slice(first // 8, last // 8)
             dst = rounded_tile(name).rearrange("p (q t e j) -> p q t j e", t=PACK, e=2, j=PACK)
             src = raw[name].rearrange("p j (q t e) -> p q t j e", t=PACK, e=2)
+            if engine == "V":
+                dst = rounded_tile(name).rearrange("p (q e j) -> p q j e", e=PACK, j=PACK)
+                src = raw[name].rearrange("p j (q e) -> p q j e", e=PACK)
+                runs = slice(first // PACK, last // PACK)
             move(engine, name, dst[:, runs], src[:, runs])
 
         def cast_slots(name, engine, first, last):
             dst = rounded_tile(name).rearrange("p (t q e j) -> p q t j e", t=PACK, e=2, j=PACK)
             src = raw[name].rearrange("p j (q t e) -> p q t j e", t=PACK, e=2)
-            move(engine, name, dst[:, :, first:last], src[:, :, first:last])
+            if last - first == PACK:
+                dst = rounded_tile(name).rearrange("p (a t q e j) -> p a q j t e", a=2, t=2, e=2, j=PACK)
+                src = raw[name].rearrange("p j (q a t e) -> p a q j t e", a=2, t=2, e=2)
+                for a in range(2):
+                    move(engine, name, dst[:, a], src[:, a])
+            else:
+                move(engine, name, dst[:, :, first:last], src[:, :, first:last])
 
         def quantize(words, plane, values):
             nc.vector.quantize_mx(out=words.bitcast(FP8X4), scales=plane, in_=values)

@@ -167,7 +167,7 @@ def tile_picked_pick_glu_silu_srt_e_kernel(tc, xT, w1, w3, w2, offs, out):
         silu_quads = {}
         up_banks = {}
 
-        def gate(g, v, over=None):
+        def gate(g, v, over=None, pairs=(0, 1)):
             if over is None:
                 tile = ring.tile([P, 2, 2 * UNIT, 2], F32, name="silu")
                 values = tile[:]
@@ -179,7 +179,7 @@ def tile_picked_pick_glu_silu_srt_e_kernel(tc, xT, w1, w3, w2, offs, out):
             half, place = divmod(2 * v * UNIT, HALF)
             words = picked_words[:, 2 * v * UNIT : (2 * v + 2) * UNIT]
             plane = picked_bytes[half][:, place : place + 2 * UNIT]
-            for pair in range(2):
+            for pair in pairs:
                 bank = acc.tile([P, 2, 2 * UNIT], F32, name="gate", tag="gate", bufs=BANKS["gate"])
                 for s in range(2):
                     t = 2 * pair + s
@@ -267,14 +267,15 @@ def tile_picked_pick_glu_silu_srt_e_kernel(tc, xT, w1, w3, w2, offs, out):
         gate(0, 3)
         for u in range(4):
             up_and_gated(1, u)
+        gate(1, 2, over="w2_0", pairs=(0,))
         cast_columns("w2_1", "S", 0, W2_SCALAR_COLUMNS)
+        gate(1, 2, over="w2_0", pairs=(1,))
         cast_columns("w2_1", "V", W2_SCALAR_COLUMNS, N)
         quantize_weights("w2_0", 0, N)
         quantize_h(1, 0, HALF)
         quantize_weights("w2_1", 0, N)
 
-        for v in range(2, 4):
-            gate(1, v, over="w2_1")
+        gate(1, 3, over="w2_1")
         up_and_gated(0, 5, "spare")
         up(1, 4)
         up(1, 5)

@@ -18,24 +18,24 @@ P = 128
 PACK = 4
 PASS = P * PACK
 UNIT = 128
-HALF = S // 2
 QUARTER = S // 4
+HALF = S // 2
 LIST_ROWS = 16
+BANK_BYTES = 2048
 FLOPS = 2 * S * (2 * K * H + H * N)
 
 TOKEN_CUTS = (0, 1024, 1536, 2048)
 LOAD_ORDER = ("x0", "offs", "x1", "x2", "w1_0", "w3_0", "w1_1", "w3_1", "w2_0", "w2_1")
-BANKS = {"gate": 3, "up": 3, "spare": 2}
-SILU_TILES = 4
-W2_SCALAR_COLUMNS = 384
+RINGS = {"gate": (0, 1, 2, 6, 7, 0, 1, 2, 6, 7, 0, 1, 2, 0, 1, 2), "up": (3, 4, 5)}
+SPAN = {"w1_0": 8192, "w3_0": 12544, "w1_1": 8192, "w3_1": 14848, "w2_0": 8192, "w2_1": 8192}
 
 
 def tile_picked_pick_glu_silu_srt_e_kernel(tc, xT, w1, w3, w2, offs, out):
     nc = tc.nc
     with ExitStack() as ctx:
         keep = ctx.enter_context(tc.tile_pool(name="keep", bufs=1))
-        ring = ctx.enter_context(tc.tile_pool(name="ring", bufs=SILU_TILES))
-        acc = ctx.enter_context(tc.psum_pool(name="acc", bufs=3))
+        placed = ctx.enter_context(tc.tile_pool(name="placed", bufs=1))
+        acc = ctx.enter_context(tc.psum_pool(name="acc", bufs=1))
 
         offsets = keep.tile([P, S // LIST_ROWS], U16, name="offsets")
         table_load = keep.tile([P, 1], F32, name="table_load")
@@ -44,6 +44,17 @@ def tile_picked_pick_glu_silu_srt_e_kernel(tc, xT, w1, w3, w2, offs, out):
         token_bytes = keep.tile([P, T], U8, name="token_bytes", align_bytes=64)
         nc.gpsimd.memset(token_bytes[:], 0)
         token_words = keep.tile([P, T], U32, name="token_words", align_bytes=64)
+
+        start_of = {}
+        for name in SPAN:
+            start_of[name] = sum(SPAN[earlier] for earlier in start_of)
+
+        def new_tile(shape, dtype, name, over=None):
+            if over is None:
+                tile = keep.tile(shape, dtype, name=name, align_bytes=64)
+            else:
+                tile = placed.tile(shape, dtype, name=name, align_bytes=64, offset=start_of[over[0]] + over[1])
+            return tile
 
         sources = {}
         for c in range(len(TOKEN_CUTS) - 1):
@@ -57,15 +68,19 @@ def tile_picked_pick_glu_silu_srt_e_kernel(tc, xT, w1, w3, w2, offs, out):
         for name in LOAD_ORDER:
             if name == "offs":
                 nc.sync.dma_start(offsets[:], offs)
+                continue
+            width = sources[name].shape[1]
+            if name in SPAN:
+                tile = new_tile([P, SPAN[name] // 4], F32, "raw_" + name, (name, 0))
             else:
-                tile = keep.tile([P, PACK, sources[name].shape[1]], F32, name="raw_" + name, tag="raw_" + name, align_bytes=64)
-                if name.startswith("w2"):
-                    dealt = sources[name].rearrange("(q t e) c -> t q e c", t=PACK, e=2)
-                    for t in range(PACK):
-                        nc.sync.dma_start(out=tile[:, t, :], in_=dealt[t])
-                else:
-                    nc.sync.dma_start(out=tile[:], in_=sources[name].rearrange("(p j) c -> p j c", j=PACK))
-                raw[name] = tile[:]
+                tile = new_tile([P, PACK * width], F32, "raw_" + name)
+            raw[name] = tile[:, 0 : PACK * width].rearrange("p (j c) -> p j c", j=PACK)
+            if name.startswith("w2"):
+                dealt = sources[name].rearrange("(q t e) c -> t q e c", t=PACK, e=2)
+                for t in range(PACK):
+                    nc.sync.dma_start(out=raw[name][:, t, :], in_=dealt[t])
+            else:
+                nc.sync.dma_start(out=raw[name], in_=sources[name].rearrange("(p j) c -> p j c", j=PACK))
 
         rounded = {}
         codes = {}
@@ -73,8 +88,7 @@ def tile_picked_pick_glu_silu_srt_e_kernel(tc, xT, w1, w3, w2, offs, out):
 
         def rounded_tile(name):
             if name not in rounded:
-                tile = keep.tile([P, PACK * sources[name].shape[1]], BF16, name="rounded_" + name, align_bytes=64)
-                rounded[name] = tile
+                rounded[name] = new_tile([P, PACK * sources[name].shape[1]], BF16, "rounded_" + name)
             return rounded[name][:]
 
         def move(engine, name, dst, src):
@@ -86,24 +100,24 @@ def tile_picked_pick_glu_silu_srt_e_kernel(tc, xT, w1, w3, w2, offs, out):
                 nc.scalar.copy(dst, src)
 
         def cast_columns(name, engine, first, last):
-            runs = slice(first // 8, last // 8)
-            dst = rounded_tile(name).rearrange("p (q t e j) -> p q t j e", t=PACK, e=2, j=PACK)
-            src = raw[name].rearrange("p j (q t e) -> p q t j e", t=PACK, e=2)
             if engine == "V":
                 dst = rounded_tile(name).rearrange("p (q e j) -> p q j e", e=PACK, j=PACK)
                 src = raw[name].rearrange("p j (q e) -> p q j e", e=PACK)
                 runs = slice(first // PACK, last // PACK)
+            else:
+                dst = rounded_tile(name).rearrange("p (q t e j) -> p q t j e", t=PACK, e=2, j=PACK)
+                src = raw[name].rearrange("p j (q t e) -> p q t j e", t=PACK, e=2)
+                runs = slice(first // 8, last // 8)
             move(engine, name, dst[:, runs], src[:, runs])
 
         def cast_slots(name, engine, first, last):
-            dst = rounded_tile(name).rearrange("p (t q e j) -> p q t j e", t=PACK, e=2, j=PACK)
-            src = raw[name].rearrange("p j (q t e) -> p q t j e", t=PACK, e=2)
-            if last - first == PACK:
+            if engine == "V" and last - first == 2:
                 dst = rounded_tile(name).rearrange("p (a t q e j) -> p a q j t e", a=2, t=2, e=2, j=PACK)
                 src = raw[name].rearrange("p j (q a t e) -> p a q j t e", a=2, t=2, e=2)
-                for a in range(2):
-                    move(engine, name, dst[:, a], src[:, a])
+                move(engine, name, dst[:, first // 2], src[:, first // 2])
             else:
+                dst = rounded_tile(name).rearrange("p (t q e j) -> p q t j e", t=PACK, e=2, j=PACK)
+                src = raw[name].rearrange("p j (q t e) -> p q t j e", t=PACK, e=2)
                 move(engine, name, dst[:, :, first:last], src[:, :, first:last])
 
         def quantize(words, plane, values):
@@ -115,33 +129,38 @@ def tile_picked_pick_glu_silu_srt_e_kernel(tc, xT, w1, w3, w2, offs, out):
 
         def quantize_weights(name, first, last):
             if name not in codes:
-                words = keep.tile([P, PASS], U32, name="codes_" + name, align_bytes=64)
-                plane = keep.tile([P, PASS], U8, name="scales_" + name, align_bytes=64)
-                codes[name] = words
-                scales[name] = plane
+                codes[name] = new_tile([P, PASS], U32, "codes_" + name)
+                scales[name] = new_tile([P, PASS], U8, "scales_" + name)
             quantize(codes[name][:, first:last], scales[name][:, first:last], rounded[name][:, first * PACK : last * PACK])
 
-        picked_words = keep.tile([P, S], U32, name="picked_words", align_bytes=64)
-        early_bytes = keep.tile([P, HALF], U8, name="early_bytes", align_bytes=64)
-        late_bytes = keep.tile([P, HALF], U8, name="late_bytes", tag="raw_w1_0", align_bytes=64)
-        picked_bytes = (early_bytes, late_bytes)
+        picked_words = new_tile([P, S], U32, "picked_words")
+        picked_bytes = {}
 
-        def gather(dst, window, half):
-            first, last = half * HALF, (half + 1) * HALF
+        def gather(dst, window, first, last):
             entries = offsets[:, first // LIST_ROWS : last // LIST_ROWS]
             nc.vector.tensor_copy(out=dst, in_=window[:, 0 : last + T - S].indirect(entries))
 
-        h_tags = ("raw_w1_1", "h_rounded1")
-        h_rounded = []
-        h_codes = []
-        h_scales = []
-        for g in range(2):
-            values = keep.tile([P, S, PACK], BF16, name="h_rounded%d" % g, tag=h_tags[g], align_bytes=64)
-            words = keep.tile([P, S], U32, name="h_codes%d" % g, align_bytes=64)
-            plane = keep.tile([P, S], U8, name="h_scales%d" % g, align_bytes=64)
-            h_rounded.append(values)
-            h_codes.append(words)
-            h_scales.append(plane)
+        def gather_words(first, last):
+            gather(picked_words[:, first:last], token_words, first, last)
+
+        def gather_bytes(first, last, over=None):
+            tile = new_tile([P, last - first], U8, "picked_bytes%d" % first, over)
+            gather(tile[:], token_bytes, first, last)
+            for place in range(first, last, UNIT):
+                picked_bytes[place] = (tile, place - first)
+
+        def tokens(first, last):
+            tile, place = picked_bytes[first]
+            return picked_words[:, first:last], tile[:, place : place + last - first]
+
+        turns = {kind: 0 for kind in RINGS}
+
+        def next_bank(kind, shape):
+            ring = RINGS[kind]
+            name = "%s%d" % (kind, turns[kind])
+            bank = acc.tile(shape, F32, name=name, offset=BANK_BYTES * ring[turns[kind] % len(ring)])
+            turns[kind] = turns[kind] + 1
+            return bank
 
         def multiply(dst, name, rows, words, plane, start, stop):
             nc.tensor.matmul_mx(
@@ -154,194 +173,209 @@ def tile_picked_pick_glu_silu_srt_e_kernel(tc, xT, w1, w3, w2, offs, out):
                 stop=stop,
             )
 
-        def unit_products(name, u, kind):
-            bank = acc.tile([P, PACK, UNIT], F32, name=kind, tag=kind, bufs=BANKS[kind])
-            half, place = divmod(u * UNIT, HALF)
-            words = picked_words[:, u * UNIT : (u + 1) * UNIT]
-            plane = picked_bytes[half][:, place : place + UNIT]
-            for t in range(PACK):
-                multiply(bank[:, t, :], name, slice(t * P, (t + 1) * P), words, plane, True, True)
-            return bank[:].rearrange("p t n -> p n t")
-
+        gate_banks = {}
         silus = {}
-        silu_quads = {}
         up_banks = {}
 
-        def gate(g, v, over=None, pairs=(0, 1)):
-            if over is None:
-                tile = ring.tile([P, 2, 2 * UNIT, 2], F32, name="silu")
-                values = tile[:]
-            else:
-                if over not in silu_quads:
-                    quad = keep.tile([P, 2, 2, 2 * UNIT, 2], F32, name="silus_" + over, tag="raw_" + over, align_bytes=64)
-                    silu_quads[over] = quad
-                values = silu_quads[over][:, v % 2]
-            half, place = divmod(2 * v * UNIT, HALF)
-            words = picked_words[:, 2 * v * UNIT : (2 * v + 2) * UNIT]
-            plane = picked_bytes[half][:, place : place + 2 * UNIT]
-            for pair in pairs:
-                bank = acc.tile([P, 2, 2 * UNIT], F32, name="gate", tag="gate", bufs=BANKS["gate"])
-                for s in range(2):
-                    t = 2 * pair + s
-                    multiply(bank[:, s, :], "w1_%d" % g, slice(t * P, (t + 1) * P), words, plane, True, True)
-                nc.scalar.activation(values[:, pair], bank[:].rearrange("p s n -> p n s"), SILU)
-            for r in range(2):
-                silus[g, 2 * v + r] = values[:, :, r * UNIT : (r + 1) * UNIT, :].rearrange("p a n s -> p n a s")
+        def gate(g, v, pair):
+            bank = next_bank("gate", [P, 2, QUARTER])
+            gate_banks[g, v, pair] = bank
+            words, plane = tokens(v * QUARTER, (v + 1) * QUARTER)
+            for s in range(2):
+                t = 2 * pair + s
+                multiply(bank[:, s, :], "w1_%d" % g, slice(t * P, (t + 1) * P), words, plane, True, True)
 
-        def up(g, u, kind="up"):
-            up_banks[g, u] = unit_products("w3_%d" % g, u, kind)
+        def silu(g, v, pair, over=None):
+            if (g, v) not in silus:
+                silus[g, v] = new_tile([P, 2, QUARTER, 2], F32, "silu%d_%d" % (g, v), over)
+            nc.scalar.activation(silus[g, v][:, pair], gate_banks[g, v, pair][:].rearrange("p s n -> p n s"), SILU)
 
-        def gated(g, u):
-            dst = h_rounded[g][:, u * UNIT : (u + 1) * UNIT, :].rearrange("p n (a s) -> p n a s", a=2)
-            nc.vector.tensor_tensor(out=dst, in0=up_banks[g, u].rearrange("p n (a s) -> p n a s", a=2), in1=silus[g, u], op=MULT)
+        def up(g, u):
+            bank = next_bank("up", [P, PACK, UNIT])
+            up_banks[g, u] = bank
+            words, plane = tokens(u * UNIT, (u + 1) * UNIT)
+            for t in range(PACK):
+                multiply(bank[:, t, :], "w3_%d" % g, slice(t * P, (t + 1) * P), words, plane, True, True)
 
-        def up_and_gated(g, u, kind="up"):
-            up(g, u, kind)
-            gated(g, u)
+        h_values = {}
+        h_words = {}
+        h_planes = {}
 
-        def quantize_h(g, first, last):
-            values = h_rounded[g][:, first:last, :].rearrange("p n t -> p (n t)")
-            quantize(h_codes[g][:, first:last], h_scales[g][:, first:last], values)
+        def gated(g, u, over=None):
+            half, place = divmod(u * UNIT, HALF)
+            if (g, half) not in h_values:
+                h_values[g, half] = new_tile([P, HALF, PACK], BF16, "h_values%d_%d" % (g, half), over)
+            dst = h_values[g, half][:, place : place + UNIT, :].rearrange("p n (a s) -> p n a s", a=2)
+            ups = up_banks[g, u][:].rearrange("p (a s) n -> p n a s", a=2)
+            first = u % 2 * UNIT
+            gates = silus[g, u // 2][:, :, first : first + UNIT, :].rearrange("p a n s -> p n a s")
+            nc.vector.tensor_tensor(out=dst, in0=ups, in1=gates, op=MULT)
 
-        def output_pass(dst, m, first, last, g, opens):
-            words, plane = h_codes[g][:, first:last], h_scales[g][:, first:last]
-            multiply(dst, "w2_%d" % g, slice(m * P, (m + 1) * P), words, plane, opens, not opens)
+        def h_operand(g, first, last):
+            half, place = divmod(first * UNIT, HALF)
+            cols = slice(place, place + (last - first) * UNIT)
+            return h_words[g, half][:, cols], h_planes[g, half][:, cols]
 
-        def store(values, m, blocks, first, last):
-            rows = out[m * P : (m + blocks) * P, first:last]
-            nc.sync.dma_start(out=rows.rearrange("(m p) n -> p m n", p=P), in_=values)
+        def quantize_h(g, first, last, over=None):
+            half, place = divmod(first * UNIT, HALF)
+            if (g, half) not in h_words:
+                h_words[g, half] = new_tile([P, HALF], U32, "h_words%d_%d" % (g, half), over)
+                h_planes[g, half] = new_tile([P, HALF], U8, "h_plane%d_%d" % (g, half))
+            values = h_values[g, half][:, place : place + (last - first) * UNIT, :].rearrange("p n t -> p (n t)")
+            quantize(*h_operand(g, first, last), values)
 
-        def output(m, blocks, first, last, kind, groups):
-            width = last - first
-            bank = acc.tile([P, blocks * width], F32, name="y_bank", tag=kind, bufs=BANKS[kind])
-            for place in range(blocks):
-                for g in groups:
-                    output_pass(bank[:, place * width : (place + 1) * width], m + place, first, last, g, g == groups[0])
-            y = keep.tile([P, blocks, width], F32, name="y%d_%d" % (first, m))
-            nc.scalar.copy(y[:].rearrange("p m n -> p (m n)"), bank[:])
-            store(y[:], m, blocks, first, last)
+        sums = {}
 
-        cast_columns("x0", "V", 0, 512)
-        cast_columns("x0", "S", 512, 1024)
-        quantize_tokens(0, 0, 512)
-        quantize_tokens(0, 512, 1024)
-        cast_columns("x1", "S", 0, 256)
-        cast_columns("x1", "V", 256, 512)
-        quantize_tokens(1, 0, 256)
-        quantize_tokens(1, 256, 512)
-        gather(picked_words[:, 0:HALF], token_words, 0)
-        gather(early_bytes[:], token_bytes, 0)
-        cast_columns("x2", "S", 0, 256)
-        cast_columns("x2", "S", 256, 512)
-        quantize_tokens(2, 0, 256)
-        quantize_tokens(2, 256, 512)
-
-        cast_slots("w1_0", "S", 0, 2)
-        cast_slots("w1_0", "S", 2, 3)
-        gather(picked_words[:, HALF:S], token_words, 1)
-        cast_slots("w1_0", "V", 3, 4)
-        quantize_weights("w1_0", 0, 256)
-        quantize_weights("w1_0", 256, 512)
-        gather(late_bytes[:], token_bytes, 1)
-        cast_slots("w3_0", "S", 0, 2)
-        cast_slots("w3_0", "V", 3, 4)
-        cast_slots("w3_0", "S", 2, 3)
-        quantize_weights("w3_0", 0, 256)
-        quantize_weights("w3_0", 256, 512)
-
-        for v in range(2):
-            gate(0, v, over="w3_0")
-        gate(0, 2)
-        cast_slots("w1_1", "V", 0, PACK)
-        up_and_gated(0, 0)
-        quantize_weights("w1_1", 0, PASS)
-        for v in range(2):
-            gate(1, v)
-        for u in range(1, 4):
-            up_and_gated(0, u)
-        cast_slots("w3_1", "V", 0, PACK)
-        up_and_gated(0, 4)
-        quantize_weights("w3_1", 0, PASS)
-        quantize_h(0, 0, HALF)
-        cast_columns("w2_0", "S", 0, N)
-        gate(0, 3)
-        for u in range(4):
-            up_and_gated(1, u)
-        gate(1, 2, over="w2_0", pairs=(0,))
-        cast_columns("w2_1", "S", 0, W2_SCALAR_COLUMNS)
-        gate(1, 2, over="w2_0", pairs=(1,))
-        cast_columns("w2_1", "V", W2_SCALAR_COLUMNS, N)
-        quantize_weights("w2_0", 0, N)
-        quantize_h(1, 0, HALF)
-        quantize_weights("w2_1", 0, N)
-
-        gate(1, 3, over="w2_1")
-        up_and_gated(0, 5, "spare")
-        up(1, 4)
-        up(1, 5)
-        up(0, 6, "spare")
-        up(0, 7, "spare")
-        banks = {}
-
-        def open_sum(m, blocks, first, last, kind, g):
-            width = last - first
-            bank = acc.tile([P, blocks * width], F32, name="y_bank", tag=kind, bufs=BANKS[kind])
-            banks[m, first] = bank
-            for place in range(blocks):
-                words, plane = h_codes[g][:, first:last], h_scales[g][:, first:last]
-                multiply(bank[:, place * width : (place + 1) * width], "w2_%d" % g, slice((m + place) * P, (m + place + 1) * P), words, plane, place == 0, False)
-
-        def close_sum(m, blocks, first, last, g, engine):
-            width = last - first
-            bank = banks[m, first]
-            for place in range(blocks):
-                words, plane = h_codes[g][:, first:last], h_scales[g][:, first:last]
-                multiply(bank[:, place * width : (place + 1) * width], "w2_%d" % g, slice((m + place) * P, (m + place + 1) * P), words, plane, False, place == blocks - 1)
-            y = keep.tile([P, blocks, width], F32, name="y%d_%d" % (first, m))
-            move(engine, "y", y[:].rearrange("p m n -> p (m n)"), bank[:])
-            store(y[:], m, blocks, first, last)
-
-        open_sum(0, 1, 0, HALF, "up", 0)
-        close_sum(0, 1, 0, HALF, 1, "S")
-
-        gated(1, 4)
-        up(1, 6)
-        gated(1, 5)
-        up(1, 7)
-        quantize_h(0, HALF, HALF + QUARTER)
-        for m in range(1, 4):
-            open_sum(m, 1, 0, HALF, "gate", 0)
-            close_sum(m, 1, 0, HALF, 1, "S")
-        gated(0, 6)
-        quantize_h(1, HALF, HALF + QUARTER)
-        gated(0, 7)
-        for m in (0, 2):
-            open_sum(m, 2, HALF, HALF + QUARTER, "spare", 0)
-        for m in (0, 2):
-            close_sum(m, 2, HALF, HALF + QUARTER, 1, "S")
-        gated(1, 6)
-        quantize_h(0, S - QUARTER, S)
-        quantize_h(1, S - QUARTER, S - UNIT)
-        gated(1, 7)
-
-        def shared_passes(bank, m, blocks, u, g):
-            cols = slice(u * UNIT, (u + 1) * UNIT)
+        def output_passes(g, m, blocks, first, last, bank=None):
+            if g == 0:
+                shape = [P, blocks, (last - first) * UNIT]
+                sums[m, first] = acc.tile(shape, F32, name="sum%d_%d" % (m, first), offset=BANK_BYTES * bank)
+            words, plane = h_operand(g, first, last)
             for place in range(blocks):
                 rows = slice((m + place) * P, (m + place + 1) * P)
                 opens, closes = g == 0 and place == 0, g == 1 and place == blocks - 1
-                multiply(bank[:, place, :], "w2_%d" % g, rows, h_codes[g][:, cols], h_scales[g][:, cols], opens, closes)
+                multiply(sums[m, first][:, place, :], "w2_%d" % g, rows, words, plane, opens, closes)
 
-        pieces = ((6, 0, 4, "up", "S"), (7, 0, 2, "gate", "V"), (7, 2, 2, "gate", "S"))
-        last_banks = []
-        for u, m, blocks, kind, engine in pieces:
-            bank = acc.tile([P, blocks, UNIT], F32, name="y_bank", tag=kind, bufs=BANKS[kind])
-            last_banks.append(bank)
-            shared_passes(bank, m, blocks, u, 0)
-        quantize_h(1, S - UNIT, S)
-        y = keep.tile([P, PACK, QUARTER], F32, name="y_last")
-        for bank, (u, m, blocks, kind, engine) in zip(last_banks, pieces):
-            shared_passes(bank, m, blocks, u, 1)
-            first = u * UNIT - (S - QUARTER)
-            move(engine, "y", y[:, m : m + blocks, first : first + UNIT], bank[:])
+        def copy_and_store(engine, m, blocks, first, last):
+            y = new_tile([P, blocks, (last - first) * UNIT], F32, "y%d_%d" % (first, m))
+            move(engine, "y", y[:], sums[m, first][:])
+            rows = out[m * P : (m + blocks) * P, first * UNIT : last * UNIT]
+            nc.sync.dma_start(out=rows.rearrange("(m p) n -> p m n", p=P), in_=y[:])
+
+        cast_columns("x0", "V", 0, 384)
+        cast_columns("x0", "V", 384, 640)
+        cast_columns("x0", "S", 640, 1024)
+        quantize_tokens(0, 0, 384)
+        quantize_tokens(0, 384, 640)
+        quantize_tokens(0, 640, 1024)
+        cast_columns("x1", "S", 256, 512)
+        cast_columns("x1", "V", 0, 256)
+        quantize_tokens(1, 0, 256)
+        quantize_tokens(1, 256, 512)
+        gather_words(0, QUARTER)
+        gather_words(QUARTER, HALF)
+        gather_bytes(0, HALF)
+        cast_columns("x2", "S", 0, 256)
+        cast_columns("x2", "S", 256, 512)
+        quantize_tokens(2, 0, 256)
+        cast_slots("w1_0", "V", 3, 4)
+        quantize_tokens(2, 256, 512)
+        cast_slots("w1_0", "S", 0, 2)
+        cast_slots("w1_0", "S", 2, 3)
+        gather_words(HALF, HALF + QUARTER)
+        gather_words(HALF + QUARTER, S)
+        quantize_weights("w1_0", 0, 256)
+        quantize_weights("w1_0", 256, 512)
+        gate(0, 0, 0)
+        gate(0, 0, 1)
+        gate(0, 1, 0)
+        gate(0, 1, 1)
+        gather_bytes(HALF, HALF + QUARTER, over=("w1_0", 0))
+        gate(0, 2, 0)
+        cast_slots("w3_0", "V", 2, 4)
+        cast_slots("w3_0", "S", 0, 2)
+        gather_bytes(HALF + QUARTER, S, over=("w3_0", 12288))
+        quantize_weights("w3_0", 0, 256)
+        quantize_weights("w3_0", 256, 512)
+
+        silu(0, 0, 0, over=("w3_0", 0))
+        gate(0, 2, 1)
+        silu(0, 0, 1)
+        up(0, 0)
+        gate(0, 3, 0)
+        silu(0, 1, 0, over=("w3_0", 4096))
+        up(0, 1)
+        gate(0, 3, 1)
+        silu(0, 1, 1)
+        up(0, 2)
+        silu(0, 2, 0, over=("w3_0", 8192))
+        silu(0, 2, 1)
+        cast_slots("w1_1", "V", 0, 2)
+        cast_slots("w1_1", "V", 2, 4)
+        gated(0, 0, over=("w1_1", 0))
+        quantize_weights("w1_1", 0, PASS)
+        silu(0, 3, 0)
+        silu(0, 3, 1)
+        up(0, 3)
+        gate(1, 0, 0)
+        gate(1, 0, 1)
+        gated(0, 1)
+        up(0, 4)
+        gate(1, 1, 0)
+        gated(0, 2)
+        gate(1, 1, 1)
+        up(0, 5)
+        cast_slots("w3_1", "S", 0, 2)
+        cast_slots("w3_1", "V", 2, 4)
+        gated(0, 3)
+        quantize_weights("w3_1", 256, 512)
+        quantize_weights("w3_1", 0, 256)
+        silu(1, 0, 0, over=("w3_1", 0))
+        up(1, 0)
+        silu(1, 0, 1)
+        silu(1, 1, 0, over=("w3_1", 4096))
+        silu(1, 1, 1)
+        gated(0, 4, over=("w3_1", 8192))
+        up(1, 1)
+        gate(1, 2, 0)
+        quantize_h(0, 0, 4, over=("w3_1", 12288))
+        gated(1, 0)
+        up(1, 2)
+        gate(1, 2, 1)
+        cast_columns("w2_0", "S", 0, N)
+        gated(1, 1)
+        up(1, 3)
+        gate(1, 3, 0)
+        cast_columns("w2_1", "V", 256, N)
+        gated(1, 2)
+        up(1, 4)
+        gated(1, 3)
+        up(1, 5)
+        gated(0, 5)
+        up(0, 6)
+        quantize_weights("w2_0", 0, N)
+        cast_columns("w2_1", "S", 0, 256)
+        output_passes(0, 0, 1, 0, 4, 6)
+        output_passes(0, 1, 1, 0, 4, 7)
+        quantize_h(1, 0, 4)
+        quantize_weights("w2_1", 0, N)
+        silu(1, 2, 0, over=("w2_1", 0))
+        gate(1, 3, 1)
+        silu(1, 2, 1)
+        output_passes(0, 2, 1, 0, 4, 0)
+        silu(1, 3, 0, over=("w2_1", 4096))
+        silu(1, 3, 1)
+        for m in range(3):
+            output_passes(1, m, 1, 0, 4)
+        quantize_h(0, 4, 6)
+        gated(1, 4)
+        up(1, 6)
+        gated(1, 5)
+        output_passes(0, 3, 1, 0, 4, 1)
+        output_passes(1, 3, 1, 0, 4)
+        up(0, 7)
+        for m in range(4):
+            copy_and_store("S", m, 1, 0, 4)
+        gated(0, 6)
+        up(1, 7)
+        quantize_h(1, 4, 6)
+        for m, bank in ((0, 2), (2, 6)):
+            output_passes(0, m, 2, 4, 6, bank)
+            output_passes(1, m, 2, 4, 6)
         for m in (0, 2):
-            store(y[:, m : m + 2, :], m, 2, S - QUARTER, S)
+            copy_and_store("S", m, 2, 4, 6)
+        gated(1, 6)
+        quantize_h(0, 6, 7)
+        gated(0, 7)
+        quantize_h(1, 6, 7)
+        output_passes(0, 0, 4, 6, 7, 7)
+        output_passes(1, 0, 4, 6, 7)
+        copy_and_store("S", 0, 4, 6, 7)
+        gated(1, 7)
+        quantize_h(0, 7, 8)
+        quantize_h(1, 7, 8)
+        for m, bank in ((0, 0), (2, 1)):
+            output_passes(0, m, 2, 7, 8, bank)
+        for m, engine in ((0, "V"), (2, "S")):
+            output_passes(1, m, 2, 7, 8)
+            copy_and_store(engine, m, 2, 7, 8)

@@ -27,7 +27,7 @@ FLOPS = 2 * S * (2 * K * H + H * N)
 TOKEN_CUTS = (0, 1024, 1536, 2048)
 LOAD_ORDER = ("x0", "offs", "x1", "x2", "w1_0", "w3_0", "w1_1", "w3_1", "w2_0", "w2_1")
 RINGS = {"gate": (0, 1, 2, 6, 7, 0, 1, 2, 6, 7, 0, 1, 2, 0, 1, 2), "up": (3, 4, 5)}
-SPAN = {"w1_0": 8192, "w3_0": 12544, "w1_1": 8192, "w3_1": 14848, "w2_0": 8192, "w2_1": 8192}
+SPAN = {"w1_0": 8192, "w3_0": 12544, "w1_1": 8192, "w3_1": 14848, "w2_0": 8192, "w2_1": 10240}
 
 
 def tile_picked_pick_glu_silu_srt_e_kernel(tc, xT, w1, w3, w2, offs, out):
@@ -267,8 +267,8 @@ def tile_picked_pick_glu_silu_srt_e_kernel(tc, xT, w1, w3, w2, offs, out):
         quantize_weights("w1_0", 0, 256)
         quantize_weights("w1_0", 256, 512)
         gate(0, 0, 0)
-        gate(0, 0, 1)
         gate(0, 1, 0)
+        gate(0, 0, 1)
         gate(0, 1, 1)
         gather_bytes(HALF, HALF + QUARTER, over=("w1_0", 0))
         gate(0, 2, 0)
@@ -280,10 +280,10 @@ def tile_picked_pick_glu_silu_srt_e_kernel(tc, xT, w1, w3, w2, offs, out):
 
         silu(0, 0, 0, over=("w3_0", 0))
         gate(0, 2, 1)
-        silu(0, 0, 1)
+        silu(0, 1, 0, over=("w3_0", 4096))
         up(0, 0)
         gate(0, 3, 0)
-        silu(0, 1, 0, over=("w3_0", 4096))
+        silu(0, 0, 1)
         up(0, 1)
         gate(0, 3, 1)
         silu(0, 1, 1)
@@ -304,7 +304,7 @@ def tile_picked_pick_glu_silu_srt_e_kernel(tc, xT, w1, w3, w2, offs, out):
         gate(1, 1, 0)
         gated(0, 2)
         gate(1, 1, 1)
-        up(0, 5)
+        gate(1, 2, 0)
         cast_slots("w3_1", "S", 0, 2)
         cast_slots("w3_1", "V", 2, 4)
         gated(0, 3)
@@ -313,26 +313,26 @@ def tile_picked_pick_glu_silu_srt_e_kernel(tc, xT, w1, w3, w2, offs, out):
         silu(1, 0, 0, over=("w3_1", 0))
         up(1, 0)
         silu(1, 0, 1)
+        up(1, 1)
         silu(1, 1, 0, over=("w3_1", 4096))
         silu(1, 1, 1)
         gated(0, 4, over=("w3_1", 8192))
-        up(1, 1)
-        gate(1, 2, 0)
-        quantize_h(0, 0, 4, over=("w3_1", 12288))
-        gated(1, 0)
         up(1, 2)
+        quantize_h(0, 0, 4, over=("w3_1", 12288))
         gate(1, 2, 1)
-        cast_columns("w2_0", "S", 0, N)
-        gated(1, 1)
+        gated(1, 0)
         up(1, 3)
         gate(1, 3, 0)
-        cast_columns("w2_1", "V", 256, N)
+        cast_columns("w2_0", "S", 0, N)
+        gated(1, 1)
+        up(0, 5)
         gated(1, 2)
         up(1, 4)
         gated(1, 3)
         up(1, 5)
         gated(0, 5)
         up(0, 6)
+        cast_columns("w2_1", "V", 256, N)
         quantize_weights("w2_0", 0, N)
         cast_columns("w2_1", "S", 0, 256)
         output_passes(0, 0, 1, 0, 4, 6)
@@ -342,12 +342,13 @@ def tile_picked_pick_glu_silu_srt_e_kernel(tc, xT, w1, w3, w2, offs, out):
         silu(1, 2, 0, over=("w2_1", 0))
         gate(1, 3, 1)
         silu(1, 2, 1)
-        output_passes(0, 2, 1, 0, 4, 0)
         silu(1, 3, 0, over=("w2_1", 4096))
         silu(1, 3, 1)
-        for m in range(3):
-            output_passes(1, m, 1, 0, 4)
-        quantize_h(0, 4, 6)
+        output_passes(1, 0, 1, 0, 4)
+        output_passes(1, 1, 1, 0, 4)
+        output_passes(0, 2, 1, 0, 4, 0)
+        output_passes(1, 2, 1, 0, 4)
+        quantize_h(0, 4, 6, over=("w2_1", 8192))
         gated(1, 4)
         up(1, 6)
         gated(1, 5)

@@ -27,7 +27,7 @@ FLOPS = 2 * S * (2 * K * H + H * N)
 TOKEN_CUTS = (0, 1024, 1536, 2048)
 LOAD_ORDER = ("x0", "offs", "x1", "x2", "w1_0", "w3_0", "w1_1", "w3_1", "w2_0", "w2_1")
 RINGS = {"gate": (0, 1, 2, 6, 7, 0, 1, 2, 6, 7, 0, 1, 2, 0, 1, 2), "up": (3, 4, 5)}
-SPAN = {"w1_0": 8192, "w3_0": 12544, "w1_1": 8192, "w3_1": 14848, "w2_0": 8192, "w2_1": 10240}
+SPAN = {"w1_0": 8192, "w3_0": 12800, "w1_1": 8192, "w3_1": 14848, "w2_0": 8192, "w2_1": 10240}
 
 
 def tile_picked_pick_glu_silu_srt_e_kernel(tc, xT, w1, w3, w2, offs, out):
@@ -88,7 +88,7 @@ def tile_picked_pick_glu_silu_srt_e_kernel(tc, xT, w1, w3, w2, offs, out):
 
         def rounded_tile(name):
             if name not in rounded:
-                rounded[name] = new_tile([P, PACK * sources[name].shape[1]], BF16, "rounded_" + name)
+                rounded[name] = new_tile([P, PACK * raw[name].shape[2]], BF16, "rounded_" + name)
             return rounded[name][:]
 
         def move(engine, name, dst, src):
@@ -131,7 +131,8 @@ def tile_picked_pick_glu_silu_srt_e_kernel(tc, xT, w1, w3, w2, offs, out):
             if name not in codes:
                 codes[name] = new_tile([P, PASS], U32, "codes_" + name)
                 scales[name] = new_tile([P, PASS], U8, "scales_" + name)
-            quantize(codes[name][:, first:last], scales[name][:, first:last], rounded[name][:, first * PACK : last * PACK])
+            values = rounded[name][:, first * PACK : last * PACK]
+            quantize(codes[name][:, first:last], scales[name][:, first:last], values)
 
         picked_words = new_tile([P, S], U32, "picked_words")
         picked_bytes = {}
@@ -227,13 +228,13 @@ def tile_picked_pick_glu_silu_srt_e_kernel(tc, xT, w1, w3, w2, offs, out):
         sums = {}
 
         def output_passes(g, m, blocks, first, last, bank=None):
-            if g == 0:
+            if bank is not None:
                 shape = [P, blocks, (last - first) * UNIT]
                 sums[m, first] = acc.tile(shape, F32, name="sum%d_%d" % (m, first), offset=BANK_BYTES * bank)
             words, plane = h_operand(g, first, last)
             for place in range(blocks):
                 rows = slice((m + place) * P, (m + place + 1) * P)
-                opens, closes = g == 0 and place == 0, g == 1 and place == blocks - 1
+                opens, closes = bank is not None and place == 0, bank is None and place == blocks - 1
                 multiply(sums[m, first][:, place, :], "w2_%d" % g, rows, words, plane, opens, closes)
 
         def copy_and_store(engine, m, blocks, first, last):
@@ -270,11 +271,10 @@ def tile_picked_pick_glu_silu_srt_e_kernel(tc, xT, w1, w3, w2, offs, out):
         gate(0, 1, 0)
         gate(0, 0, 1)
         gate(0, 1, 1)
-        gather_bytes(HALF, HALF + QUARTER, over=("w1_0", 0))
-        gate(0, 2, 0)
         cast_slots("w3_0", "V", 2, 4)
         cast_slots("w3_0", "S", 0, 2)
-        gather_bytes(HALF + QUARTER, S, over=("w3_0", 12288))
+        gather_bytes(HALF, S, over=("w3_0", 12288))
+        gate(0, 2, 0)
         quantize_weights("w3_0", 0, 256)
         quantize_weights("w3_0", 256, 512)
 
@@ -292,8 +292,9 @@ def tile_picked_pick_glu_silu_srt_e_kernel(tc, xT, w1, w3, w2, offs, out):
         silu(0, 2, 1)
         cast_slots("w1_1", "V", 0, 2)
         cast_slots("w1_1", "V", 2, 4)
+        quantize_weights("w1_1", 0, 256)
         gated(0, 0, over=("w1_1", 0))
-        quantize_weights("w1_1", 0, PASS)
+        quantize_weights("w1_1", 256, PASS)
         silu(0, 3, 0)
         silu(0, 3, 1)
         up(0, 3)
@@ -332,9 +333,9 @@ def tile_picked_pick_glu_silu_srt_e_kernel(tc, xT, w1, w3, w2, offs, out):
         up(1, 5)
         gated(0, 5)
         up(0, 6)
-        cast_columns("w2_1", "V", 256, N)
+        cast_columns("w2_1", "V", 192, N)
         quantize_weights("w2_0", 0, N)
-        cast_columns("w2_1", "S", 0, 256)
+        cast_columns("w2_1", "S", 0, 192)
         output_passes(0, 0, 1, 0, 4, 6)
         output_passes(0, 1, 1, 0, 4, 7)
         quantize_h(1, 0, 4)

@@ -76,9 +76,9 @@ def tile_picked_pick_glu_silu_srt_e_kernel(tc, xT, w1, w3, w2, offs, out):
                 tile = new_tile([P, PACK * width], F32, "raw_" + name)
             raw[name] = tile[:, 0 : PACK * width].rearrange("p (j c) -> p j c", j=PACK)
             if name.startswith("w2"):
-                dealt = sources[name].rearrange("(q t e) c -> t q e c", t=PACK, e=2)
-                for t in range(PACK):
-                    nc.sync.dma_start(out=raw[name][:, t, :], in_=dealt[t])
+                dealt = sources[name].rearrange("(q a e b) c -> a q e (b c)", a=2, e=2, b=2)
+                for a in range(2):
+                    nc.sync.dma_start(out=tile[:, 2 * a * width : 2 * (a + 1) * width], in_=dealt[a])
             else:
                 nc.sync.dma_start(out=raw[name], in_=sources[name].rearrange("(p j) c -> p j c", j=PACK))
 
@@ -111,14 +111,11 @@ def tile_picked_pick_glu_silu_srt_e_kernel(tc, xT, w1, w3, w2, offs, out):
             move(engine, name, dst[:, runs], src[:, runs])
 
         def cast_slots(name, engine, first, last):
-            if engine == "V" and last - first == 2:
-                dst = rounded_tile(name).rearrange("p (a t q e j) -> p a q j t e", a=2, t=2, e=2, j=PACK)
-                src = raw[name].rearrange("p j (q a t e) -> p a q j t e", a=2, t=2, e=2)
-                move(engine, name, dst[:, first // 2], src[:, first // 2])
-            else:
-                dst = rounded_tile(name).rearrange("p (t q e j) -> p q t j e", t=PACK, e=2, j=PACK)
-                src = raw[name].rearrange("p j (q t e) -> p q t j e", t=PACK, e=2)
-                move(engine, name, dst[:, :, first:last], src[:, :, first:last])
+            dst = rounded_tile(name).rearrange("p (a b q e j) -> p a q j b e", a=2, b=2, e=2, j=PACK)
+            src = raw[name].rearrange("p j (q a e b) -> p a q j b e", a=2, e=2, b=2)
+            a, b = divmod(first, 2)
+            places = slice(b, b + last - first)
+            move(engine, name, dst[:, a, :, :, places], src[:, a, :, :, places])
 
         def quantize(words, plane, values):
             nc.vector.quantize_mx(out=words.bitcast(FP8X4), scales=plane, in_=values)

@@ -27,7 +27,8 @@ FLOPS = 2 * S * (2 * K * H + H * N)
 TOKEN_CUTS = (0, 1024, 1536, 2048)
 LOAD_ORDER = ("x0", "offs", "x1", "x2", "w1_0", "w3_0", "w1_1", "w3_1", "w2_0", "w2_1")
 RINGS = {"gate": (0, 1, 2, 6, 7, 0, 1, 2, 6, 7, 0, 1, 2, 0, 1, 2), "up": (3, 4, 5)}
-SPAN = {"w1_0": 8192, "w3_0": 12800, "w1_1": 8192, "w3_1": 14848, "w2_0": 8192, "w2_1": 10240}
+WEIGHT_BYTES = 4 * PACK * PASS
+MARGINS = {"w1_0": 0, "w3_0": 3072, "w1_1": 0, "w3_1": 3072, "w2_0": 0, "w2_1": 3072}
 
 
 def tile_picked_pick_glu_silu_srt_e_kernel(tc, xT, w1, w3, w2, offs, out):
@@ -46,8 +47,8 @@ def tile_picked_pick_glu_silu_srt_e_kernel(tc, xT, w1, w3, w2, offs, out):
         token_words = keep.tile([P, T], U32, name="token_words", align_bytes=64)
 
         start_of = {}
-        for name in SPAN:
-            start_of[name] = sum(SPAN[earlier] for earlier in start_of)
+        for name in MARGINS:
+            start_of[name] = sum(WEIGHT_BYTES + 2 * MARGINS[earlier] for earlier in start_of) + MARGINS[name]
 
         def new_tile(shape, dtype, name, over=None):
             if over is None:
@@ -70,11 +71,8 @@ def tile_picked_pick_glu_silu_srt_e_kernel(tc, xT, w1, w3, w2, offs, out):
                 nc.sync.dma_start(offsets[:], offs)
                 continue
             width = sources[name].shape[1]
-            if name in SPAN:
-                tile = new_tile([P, SPAN[name] // 4], F32, "raw_" + name, (name, 0))
-            else:
-                tile = new_tile([P, PACK * width], F32, "raw_" + name)
-            raw[name] = tile[:, 0 : PACK * width].rearrange("p (j c) -> p j c", j=PACK)
+            tile = new_tile([P, PACK * width], F32, "raw_" + name, (name, 0) if name in MARGINS else None)
+            raw[name] = tile[:].rearrange("p (j c) -> p j c", j=PACK)
             if name.startswith("w2"):
                 dealt = sources[name].rearrange("(q a e b) c -> a q e (b c)", a=2, e=2, b=2)
                 for a in range(2):
@@ -270,14 +268,14 @@ def tile_picked_pick_glu_silu_srt_e_kernel(tc, xT, w1, w3, w2, offs, out):
         gate(0, 1, 1)
         cast_slots("w3_0", "V", 2, 4)
         cast_slots("w3_0", "S", 0, 2)
-        gather_bytes(HALF, S, over=("w3_0", 12288))
+        gather_bytes(HALF, S, over=("w3_0", 6144))
         gate(0, 2, 0)
         quantize_weights("w3_0", 0, 256)
         quantize_weights("w3_0", 256, 512)
 
-        silu(0, 0, 0, over=("w3_0", 0))
+        silu(0, 0, 0, over=("w3_0", -2048))
         gate(0, 2, 1)
-        silu(0, 1, 0, over=("w3_0", 4096))
+        silu(0, 1, 0, over=("w3_0", 2048))
         up(0, 0)
         gate(0, 3, 0)
         silu(0, 0, 1)
@@ -285,7 +283,7 @@ def tile_picked_pick_glu_silu_srt_e_kernel(tc, xT, w1, w3, w2, offs, out):
         gate(0, 3, 1)
         silu(0, 1, 1)
         up(0, 2)
-        silu(0, 2, 0, over=("w3_0", 8192))
+        silu(0, 2, 0, over=("w3_0", 6656))
         silu(0, 2, 1)
         cast_slots("w1_1", "V", 0, 2)
         cast_slots("w1_1", "V", 2, 4)
@@ -308,15 +306,15 @@ def tile_picked_pick_glu_silu_srt_e_kernel(tc, xT, w1, w3, w2, offs, out):
         gated(0, 3)
         quantize_weights("w3_1", 256, 512)
         quantize_weights("w3_1", 0, 256)
-        silu(1, 0, 0, over=("w3_1", 0))
+        silu(1, 0, 0, over=("w3_1", -3072))
         up(1, 0)
         silu(1, 0, 1)
         up(1, 1)
-        silu(1, 1, 0, over=("w3_1", 4096))
+        silu(1, 1, 0, over=("w3_1", 3072))
         silu(1, 1, 1)
-        gated(0, 4, over=("w3_1", 8192))
+        gated(0, 4, over=("w3_1", 7168))
         up(1, 2)
-        quantize_h(0, 0, 4, over=("w3_1", 12288))
+        quantize_h(0, 0, 4, over=("w3_1", 1024))
         gate(1, 2, 1)
         gated(1, 0)
         up(1, 3)
@@ -337,7 +335,7 @@ def tile_picked_pick_glu_silu_srt_e_kernel(tc, xT, w1, w3, w2, offs, out):
         output_passes(0, 1, 1, 0, 4, 7)
         quantize_h(1, 0, 4)
         quantize_weights("w2_1", 0, N)
-        silu(1, 2, 0, over=("w2_1", 0))
+        silu(1, 2, 0, over=("w2_1", -2048))
         gate(1, 3, 1)
         silu(1, 2, 1)
         silu(1, 3, 0, over=("w2_1", 4096))
@@ -346,7 +344,7 @@ def tile_picked_pick_glu_silu_srt_e_kernel(tc, xT, w1, w3, w2, offs, out):
         output_passes(1, 1, 1, 0, 4)
         output_passes(0, 2, 1, 0, 4, 0)
         output_passes(1, 2, 1, 0, 4)
-        quantize_h(0, 4, 6, over=("w2_1", 8192))
+        quantize_h(0, 4, 6, over=("w2_1", 2048))
         gated(1, 4)
         up(1, 6)
         gated(1, 5)

from contextlib import ExitStack

import concourse.mybir as mybir

K, T, S, H, N = 512, 2048, 1024, 1024, 512

F32 = mybir.dt.float32
BF16 = mybir.dt.bfloat16
U32 = mybir.dt.uint32
U16 = mybir.dt.uint16
U8 = mybir.dt.uint8
FP8X4 = mybir.dt.float8_e4m3fn_x4
COPY = mybir.ActivationFunctionType.Copy
SILU = mybir.ActivationFunctionType.Silu
MULT = mybir.AluOpType.mult

P = 128
PACK = 4
PASS = P * PACK
UNIT = 128
QUARTER = S // 4
HALF = S // 2
LIST_ROWS = 16
BANK_BYTES = 2048
FLOPS = 2 * S * (2 * K * H + H * N)

TOKEN_CUTS = (0, 1024, 1536, 2048)
LOAD_ORDER = ("x0", "offs", "x1", "x2", "w1_0", "w3_0", "w1_1", "w3_1", "w2_0", "w2_1")
RINGS = {"gate": (0, 1, 2, 6, 7, 0, 1, 2, 6, 7, 0, 1, 2, 0, 1, 2), "up": (3, 4, 5)}
WEIGHT_BYTES = 4 * PACK * PASS
MARGINS = {"w1_0": 0, "w3_0": 3072, "w1_1": 0, "w3_1": 3072, "w2_0": 0, "w2_1": 3072}


def tile_picked_pick_glu_silu_srt_e_kernel(tc, xT, w1, w3, w2, offs, out):
    nc = tc.nc
    with ExitStack() as ctx:
        keep = ctx.enter_context(tc.tile_pool(name="keep", bufs=1))
        placed = ctx.enter_context(tc.tile_pool(name="placed", bufs=1))
        acc = ctx.enter_context(tc.psum_pool(name="acc", bufs=1))

        offsets = keep.tile([P, S // LIST_ROWS], U16, name="offsets")
        table_load = keep.tile([P, 1], F32, name="table_load")
        nc.vector.memset(table_load[:], 0.0)
        nc.scalar.activation(table_load[:], table_load[:], SILU)
        token_bytes = keep.tile([P, T], U8, name="token_bytes", align_bytes=64)
        nc.gpsimd.memset(token_bytes[:], 0)
        token_words = keep.tile([P, T], U32, name="token_words", align_bytes=64)

        start_of = {}
        for name in MARGINS:
            start_of[name] = sum(WEIGHT_BYTES + 2 * MARGINS[earlier] for earlier in start_of) + MARGINS[name]

        def new_tile(shape, dtype, name, over=None):
            if over is None:
                tile = keep.tile(shape, dtype, name=name, align_bytes=64)
            else:
                tile = placed.tile(shape, dtype, name=name, align_bytes=64, offset=start_of[over[0]] + over[1])
            return tile

        sources = {}
        for c in range(len(TOKEN_CUTS) - 1):
            sources["x%d" % c] = xT[:, TOKEN_CUTS[c] : TOKEN_CUTS[c + 1]]
        for g in range(2):
            sources["w1_%d" % g] = w1[:, g * PASS : (g + 1) * PASS]
            sources["w3_%d" % g] = w3[:, g * PASS : (g + 1) * PASS]
            sources["w2_%d" % g] = w2[g * PASS : (g + 1) * PASS, :]

        raw = {}
        for name in LOAD_ORDER:
            if name == "offs":
                nc.sync.dma_start(offsets[:], offs)
                continue
            width = sources[name].shape[1]
            tile = new_tile([P, PACK * width], F32, "raw_" + name, (name, 0) if name in MARGINS else None)
            raw[name] = tile[:].rearrange("p (j c) -> p j c", j=PACK)
            if name.startswith("w2"):
                dealt = sources[name].rearrange("(q a e b) c -> a q e (b c)", a=2, e=2, b=2)
                for a in range(2):
                    nc.sync.dma_start(out=tile[:, 2 * a * width : 2 * (a + 1) * width], in_=dealt[a])
            else:
                nc.sync.dma_start(out=raw[name], in_=sources[name].rearrange("(p j) c -> p j c", j=PACK))

        rounded = {}
        codes = {}
        scales = {}

        def rounded_tile(name):
            if name not in rounded:
                rounded[name] = new_tile([P, PACK * raw[name].shape[2]], BF16, "rounded_" + name)
            return rounded[name][:]

        def move(engine, name, dst, src):
            if engine == "V":
                nc.vector.tensor_copy(out=dst, in_=src)
            elif name.startswith("x"):
                nc.scalar.activation(dst, src, COPY)
            else:
                nc.scalar.copy(dst, src)

        def cast_columns(name, engine, first, last):
            if engine == "V":
                dst = rounded_tile(name).rearrange("p (q e j) -> p q j e", e=PACK, j=PACK)
                src = raw[name].rearrange("p j (q e) -> p q j e", e=PACK)
                runs = slice(first // PACK, last // PACK)
            else:
                dst = rounded_tile(name).rearrange("p (q t e j) -> p q t j e", t=PACK, e=2, j=PACK)
                src = raw[name].rearrange("p j (q t e) -> p q t j e", t=PACK, e=2)
                runs = slice(first // 8, last // 8)
            move(engine, name, dst[:, runs], src[:, runs])

        def cast_slots(name, engine, first, last):
            dst = rounded_tile(name).rearrange("p (a b q e j) -> p a q j b e", a=2, b=2, e=2, j=PACK)
            src = raw[name].rearrange("p j (q a e b) -> p a q j b e", a=2, e=2, b=2)
            a, b = divmod(first, 2)
            places = slice(b, b + last - first)
            move(engine, name, dst[:, a, :, :, places], src[:, a, :, :, places])

        def quantize(words, plane, values):
            nc.vector.quantize_mx(out=words.bitcast(FP8X4), scales=plane, in_=values)

        def quantize_tokens(c, first, last):
            cols = slice(TOKEN_CUTS[c] + first, TOKEN_CUTS[c] + last)
            quantize(token_words[:, cols], token_bytes[:, cols], rounded["x%d" % c][:, first * PACK : last * PACK])

        def quantize_weights(name, first, last):
            if name not in codes:
                codes[name] = new_tile([P, PASS], U32, "codes_" + name)
                scales[name] = new_tile([P, PASS], U8, "scales_" + name)
            values = rounded[name][:, first * PACK : last * PACK]
            quantize(codes[name][:, first:last], scales[name][:, first:last], values)

        picked_words = new_tile([P, S], U32, "picked_words")
        picked_bytes = {}

        def gather(dst, window, first, last):
            entries = offsets[:, first // LIST_ROWS : last // LIST_ROWS]
            nc.vector.tensor_copy(out=dst, in_=window[:, 0 : last + T - S].indirect(entries))

        def gather_words(first, last):
            gather(picked_words[:, first:last], token_words, first, last)

        def gather_bytes(first, last, over=None):
            tile = new_tile([P, last - first], U8, "picked_bytes%d" % first, over)
            gather(tile[:], token_bytes, first, last)
            for place in range(first, last, UNIT):
                picked_bytes[place] = (tile, place - first)

        def tokens(first, last):
            tile, place = picked_bytes[first]
            return picked_words[:, first:last], tile[:, place : place + last - first]

        turns = {kind: 0 for kind in RINGS}

        def next_bank(kind, shape):
            ring = RINGS[kind]
            name = "%s%d" % (kind, turns[kind])
            bank = acc.tile(shape, F32, name=name, offset=BANK_BYTES * ring[turns[kind] % len(ring)])
            turns[kind] = turns[kind] + 1
            return bank

        def multiply(dst, name, rows, words, plane, start, stop):
            nc.tensor.matmul_mx(
                out=dst,
                lhsT=codes[name][:, rows].bitcast(FP8X4),
                lhsT_scale=scales[name][:, rows],
                rhs=words.bitcast(FP8X4),
                rhs_scale=plane,
                start=start,
                stop=stop,
            )

        gate_banks = {}
        silus = {}
        up_banks = {}

        def gate(g, v, pair):
            bank = next_bank("gate", [P, 2, QUARTER])
            gate_banks[g, v, pair] = bank
            words, plane = tokens(v * QUARTER, (v + 1) * QUARTER)
            for s in range(2):
                t = 2 * pair + s
                multiply(bank[:, s, :], "w1_%d" % g, slice(t * P, (t + 1) * P), words, plane, True, True)

        def silu(g, v, pair, over=None):
            if (g, v) not in silus:
                silus[g, v] = new_tile([P, 2, QUARTER, 2], F32, "silu%d_%d" % (g, v), over)
            nc.scalar.activation(silus[g, v][:, pair], gate_banks[g, v, pair][:].rearrange("p s n -> p n s"), SILU)

        def up(g, u):
            bank = next_bank("up", [P, PACK, UNIT])
            up_banks[g, u] = bank
            words, plane = tokens(u * UNIT, (u + 1) * UNIT)
            for t in range(PACK):
                multiply(bank[:, t, :], "w3_%d" % g, slice(t * P, (t + 1) * P), words, plane, True, True)

        h_values = {}
        h_words = {}
        h_planes = {}

        def gated(g, u, over=None):
            half, place = divmod(u * UNIT, HALF)
            if (g, half) not in h_values:
                h_values[g, half] = new_tile([P, HALF, PACK], BF16, "h_values%d_%d" % (g, half), over)
            dst = h_values[g, half][:, place : place + UNIT, :].rearrange("p n (a s) -> p n a s", a=2)
            ups = up_banks[g, u][:].rearrange("p (a s) n -> p n a s", a=2)
            first = u % 2 * UNIT
            gates = silus[g, u // 2][:, :, first : first + UNIT, :].rearrange("p a n s -> p n a s")
            nc.vector.tensor_tensor(out=dst, in0=ups, in1=gates, op=MULT)

        def h_operand(g, first, last):
            half, place = divmod(first * UNIT, HALF)
            cols = slice(place, place + (last - first) * UNIT)
            return h_words[g, half][:, cols], h_planes[g, half][:, cols]

        def quantize_h(g, first, last, over=None):
            half, place = divmod(first * UNIT, HALF)
            if (g, half) not in h_words:
                h_words[g, half] = new_tile([P, HALF], U32, "h_words%d_%d" % (g, half), over)
                h_planes[g, half] = new_tile([P, HALF], U8, "h_plane%d_%d" % (g, half))
            values = h_values[g, half][:, place : place + (last - first) * UNIT, :].rearrange("p n t -> p (n t)")
            quantize(*h_operand(g, first, last), values)

        sums = {}

        def output_passes(g, m, blocks, first, last, bank=None):
            if bank is not None:
                shape = [P, blocks, (last - first) * UNIT]
                sums[m, first] = acc.tile(shape, F32, name="sum%d_%d" % (m, first), offset=BANK_BYTES * bank)
            words, plane = h_operand(g, first, last)
            for place in range(blocks):
                rows = slice((m + place) * P, (m + place + 1) * P)
                opens, closes = bank is not None and place == 0, bank is None and place == blocks - 1
                multiply(sums[m, first][:, place, :], "w2_%d" % g, rows, words, plane, opens, closes)

        def copy_and_store(engine, m, blocks, first, last):
            y = new_tile([P, blocks, (last - first) * UNIT], F32, "y%d_%d" % (first, m))
            move(engine, "y", y[:], sums[m, first][:])
            rows = out[m * P : (m + blocks) * P, first * UNIT : last * UNIT]
            nc.sync.dma_start(out=rows.rearrange("(m p) n -> p m n", p=P), in_=y[:])

        cast_columns("x0", "V", 0, 384)
        cast_columns("x0", "V", 384, 640)
        cast_columns("x0", "S", 640, 1024)
        quantize_tokens(0, 0, 384)
        quantize_tokens(0, 384, 640)
        quantize_tokens(0, 640, 1024)
        cast_columns("x1", "S", 256, 512)
        cast_columns("x1", "V", 0, 256)
        quantize_tokens(1, 0, 256)
        quantize_tokens(1, 256, 512)
        gather_words(0, QUARTER)
        gather_words(QUARTER, HALF)
        gather_bytes(0, HALF)
        cast_columns("x2", "S", 0, 256)
        cast_columns("x2", "S", 256, 512)
        quantize_tokens(2, 0, 256)
        cast_slots("w1_0", "V", 3, 4)
        quantize_tokens(2, 256, 512)
        cast_slots("w1_0", "S", 0, 2)
        cast_slots("w1_0", "S", 2, 3)
        gather_words(HALF, HALF + QUARTER)
        gather_words(HALF + QUARTER, S)
        quantize_weights("w1_0", 0, 256)
        quantize_weights("w1_0", 256, 512)
        gate(0, 0, 0)
        gate(0, 1, 0)
        gate(0, 0, 1)
        gate(0, 1, 1)
        cast_slots("w3_0", "V", 2, 4)
        cast_slots("w3_0", "S", 0, 2)
        gather_bytes(HALF, S, over=("w3_0", 6144))
        gate(0, 2, 0)
        quantize_weights("w3_0", 0, 256)
        quantize_weights("w3_0", 256, 512)

        silu(0, 0, 0, over=("w3_0", -2048))
        gate(0, 2, 1)
        silu(0, 1, 0, over=("w3_0", 2048))
        up(0, 0)
        gate(0, 3, 0)
        silu(0, 0, 1)
        up(0, 1)
        gate(0, 3, 1)
        silu(0, 1, 1)
        up(0, 2)
        silu(0, 2, 0, over=("w3_0", 6656))
        silu(0, 2, 1)
        cast_slots("w1_1", "V", 0, 2)
        cast_slots("w1_1", "V", 2, 4)
        quantize_weights("w1_1", 0, 256)
        gated(0, 0, over=("w1_1", 0))
        quantize_weights("w1_1", 256, PASS)
        silu(0, 3, 0)
        silu(0, 3, 1)
        up(0, 3)
        gate(1, 0, 0)
        gate(1, 0, 1)
        gated(0, 1)
        up(0, 4)
        gate(1, 1, 0)
        gated(0, 2)
        gate(1, 1, 1)
        gate(1, 2, 0)
        cast_slots("w3_1", "S", 0, 2)
        cast_slots("w3_1", "V", 2, 4)
        gated(0, 3)
        quantize_weights("w3_1", 256, 512)
        quantize_weights("w3_1", 0, 256)
        silu(1, 0, 0, over=("w3_1", -3072))
        up(1, 0)
        silu(1, 0, 1)
        up(1, 1)
        silu(1, 1, 0, over=("w3_1", 3072))
        silu(1, 1, 1)
        gated(0, 4, over=("w3_1", 7168))
        up(1, 2)
        quantize_h(0, 0, 4, over=("w3_1", 1024))
        gate(1, 2, 1)
        gated(1, 0)
        up(1, 3)
        gate(1, 3, 0)
        cast_columns("w2_0", "S", 0, N)
        gated(1, 1)
        up(0, 5)
        gated(1, 2)
        up(1, 4)
        gated(1, 3)
        up(1, 5)
        gated(0, 5)
        up(0, 6)
        cast_columns("w2_1", "V", 192, N)
        quantize_weights("w2_0", 0, N)
        cast_columns("w2_1", "S", 0, 192)
        output_passes(0, 0, 1, 0, 4, 6)
        output_passes(0, 1, 1, 0, 4, 7)
        quantize_h(1, 0, 4)
        quantize_weights("w2_1", 0, N)
        silu(1, 2, 0, over=("w2_1", -2048))
        gate(1, 3, 1)
        silu(1, 2, 1)
        silu(1, 3, 0, over=("w2_1", 4096))
        silu(1, 3, 1)
        output_passes(1, 0, 1, 0, 4)
        output_passes(1, 1, 1, 0, 4)
        output_passes(0, 2, 1, 0, 4, 0)
        output_passes(1, 2, 1, 0, 4)
        quantize_h(0, 4, 6, over=("w2_1", 2048))
        gated(1, 4)
        up(1, 6)
        gated(1, 5)
        output_passes(0, 3, 1, 0, 4, 1)
        output_passes(1, 3, 1, 0, 4)
        up(0, 7)
        for m in range(4):
            copy_and_store("S", m, 1, 0, 4)
        gated(0, 6)
        up(1, 7)
        quantize_h(1, 4, 6)
        for m, bank in ((0, 2), (2, 6)):
            output_passes(0, m, 2, 4, 6, bank)
            output_passes(1, m, 2, 4, 6)
        for m in (0, 2):
            copy_and_store("S", m, 2, 4, 6)
        gated(1, 6)
        quantize_h(0, 6, 7)
        gated(0, 7)
        quantize_h(1, 6, 7)
        output_passes(0, 0, 4, 6, 7, 7)
        output_passes(1, 0, 4, 6, 7)
        copy_and_store("S", 0, 4, 6, 7)
        gated(1, 7)
        quantize_h(0, 7, 8)
        quantize_h(1, 7, 8)
        for m, bank in ((0, 0), (2, 1)):
            output_passes(0, m, 2, 7, 8, bank)
        for m, engine in ((0, "V"), (2, "S")):
            output_passes(1, m, 2, 7, 8)
            copy_and_store(engine, m, 2, 7, 8)
